import numpy as np
import ml_dtypes


def mxq(x, axis, fmt="e4m3"):
    dtype, down = {"e4m3": (ml_dtypes.float8_e4m3fn, 7), "e5m2": (ml_dtypes.float8_e5m2, 14)}[fmt]
    v = np.moveaxis(np.asarray(x, np.float32).astype(ml_dtypes.bfloat16).astype(np.float64), axis, -1)
    blocks = v.reshape(v.shape[:-1] + (-1, 32))
    amax = np.abs(blocks).max(-1, keepdims=True)
    byte = np.maximum(np.where(amax > 0, np.frexp(amax)[1] - 1 + 127, 0) - down, 1)
    scale = np.exp2(byte - 127.0)
    codes = (blocks / scale).astype(np.float32).astype(dtype).astype(np.float64)
    return np.moveaxis((codes * scale).reshape(v.shape), -1, axis)


WIDE = False


def mx_kscale(k):
    if not WIDE:
        return np.ones(k)
    levels = np.array([10, -10, 5, -5, 0])
    if k % 512:
        return np.exp2(np.random.permutation(np.resize(levels, k // 32))).repeat(32)
    a = np.empty((k // 512, 16))
    for p in range(k // 512):
        a[p, :8] = np.random.permutation(np.resize(levels, 8))
        for g in range(8):
            far = levels[np.abs(levels - a[p, g]) >= 10]
            a[p, g + 8] = far[np.random.randint(len(far))]
    return np.exp2(a.ravel()).repeat(32)


def f64(x):
    return np.asarray(x).astype(np.float64)


def striped(idx):
    return np.tile(np.asarray(idx).reshape(-1, 16).T, (8, 1)).astype(np.uint16)


def unstriped(offs):
    return offs[:16].T.reshape(-1).astype(np.int64)


E2M1 = np.array([0.0, 0.5, 1.0, 1.5, 2.0, 3.0, 4.0, 6.0, -0.0, -0.5, -1.0, -1.5, -2.0, -3.0, -4.0, -6.0])


def pack_weight(w, fmt):
    k, n = w.shape
    w = f64(np.asarray(w, np.float32).astype(ml_dtypes.bfloat16)).reshape(k // 32, 32, n)
    amax = np.abs(w).max(1)
    if fmt == "e4m3":
        byte = np.frexp(amax)[1] - 1 + 127 - 7
    else:
        mant, ex = np.frexp(amax / 6.0)
        byte = np.where(mant > 0.5, ex, ex - 1) + 127
    byte = np.clip(np.where(amax > 0, byte, 1), 1, 254)
    scaled = (w * np.exp2(127.0 - byte)[:, None, :]).reshape(k, n).astype(np.float32)
    by_word = np.ascontiguousarray(scaled.reshape(k // 512, 128, 4, n).transpose(0, 1, 3, 2))
    if fmt == "e4m3":
        words = by_word.astype(ml_dtypes.float8_e4m3fn).view(np.uint8)
    else:
        c = by_word.astype(ml_dtypes.float4_e2m1fn).view(np.uint8) & 0xF
        words = (c[..., 0::2] | (c[..., 1::2] << 4)).reshape(k // 512, 128, 2 * n)
    return np.ascontiguousarray(words), np.ascontiguousarray(byte.astype(np.uint8).reshape(k // 512, 16, n))


def unpack_weight(words, scales, fmt):
    g, _, n = scales.shape
    words = np.ascontiguousarray(words).reshape(g, 128, n, -1)
    if fmt == "e4m3":
        vals = words.view(ml_dtypes.float8_e4m3fn).astype(np.float64)
    else:
        nib = np.empty((g, 128, n, 4), np.uint8)
        nib[..., 0::2] = words & 0xF
        nib[..., 1::2] = words >> 4
        vals = E2M1[nib]
    vals = vals * np.repeat(np.exp2(scales.astype(np.float64) - 127.0), 8, axis=1)[..., None]
    return vals.transpose(0, 1, 3, 2).reshape(g * 512, n)


D, T, I, Q, E = 512, 2048, 512, 128, 512


def setup_inputs():
    n = np.random.standard_normal
    idx = np.random.permutation(T)[:I]
    fd = mx_kscale(D)
    fi = mx_kscale(I)
    ti = np.ones(T)
    ti[idx] = fi
    ptsp = pack_weight(n((D, T)) / fd[:, None], "e4m3")
    return {
        "query": (n((D, Q)) * 0.25 / np.sqrt(D) * fd[:, None]).astype(np.float32),
        "pts_words": ptsp[0],
        "pts_scales": ptsp[1],
        "kn": np.tile(np.random.uniform(0.5, 1.5, T), (128, 1)).astype(np.float32),
        "qn": (np.random.uniform(0.5, 1.5, (Q, 1))).astype(np.float32),
        "us": (np.random.uniform(0.5, 2.0, (1, I)) * fi).astype(np.float32),
        "coef": (n((E, T)) / ti).astype(np.float32),
        "offs": striped(idx),
    }


def reference(query, pts_words, pts_scales, kn, qn, us, coef, offs):
    idx = unstriped(offs)
    ptsu = unpack_weight(pts_words, pts_scales, "e4m3")
    queryq = mxq(f64(query), 0, "e4m3")
    ptsidxg = ptsu[:, idx]
    a = queryq.T @ ptsidxg
    w = np.exp(a - f64(qn) - f64(kn)[:1][:, idx]) * f64(us)
    wt = w.T
    vt = f64(coef)[:, idx].T
    wtq = mxq(wt, 0, "e4m3")
    vtq = mxq(vt, 0, "e4m3")
    o = wtq.T @ vtq
    return o

@@ -1,0 +1,134 @@
+from contextlib import ExitStack
+
+import concourse.mybir as mybir
+from concourse.masks import make_identity
+
+D, T, I, Q, E = 512, 2048, 512, 128, 512
+FLOPS = 2 * Q * I * D + 2 * Q * I * E
+BYTES = 4 * D * Q + D * T + 16 * T + 4 * T + 4 * Q + 4 * I + 4 * E * T + 2 * 128 * 32 + 4 * Q * E
+
+F32 = mybir.dt.float32
+BF16 = mybir.dt.bfloat16
+I32 = mybir.dt.int32
+U32 = mybir.dt.uint32
+U16 = mybir.dt.uint16
+U8 = mybir.dt.uint8
+FP8X4 = mybir.dt.float8_e4m3fn_x4
+ACT = mybir.ActivationFunctionType
+MULT = mybir.AluOpType.mult
+
+P = 128
+PACK = 4
+KN_ROW = P - 1
+E_TILES = E // P
+
+
+def tile_attend_kernelridge_kernel(tc, query, pts_words, pts_scales, kn, qn, us, coef, offs, out):
+    nc = tc.nc
+    with ExitStack() as ctx:
+        keep = ctx.enter_context(tc.tile_pool(name="keep", bufs=1))
+        psum = ctx.enter_context(tc.psum_pool(name="psum", bufs=1))
+        psum_ring = ctx.enter_context(tc.psum_pool(name="psum_ring", bufs=2))
+
+        offsets = keep.tile([P, I // 16], U16, name="offsets")
+        words = keep.tile([P, T], U32, name="words", tag="words")
+        scales = keep.tile([P, T], U8, name="scales", tag="scales")
+        kn_win = keep.tile([P, T], F32, name="kn_win", tag="kn_win")
+        q_raw = keep.tile([P, PACK, Q], F32, name="q_raw")
+        qn_col = keep.tile([P, 1], F32, name="qn_col")
+        us_cols = keep.tile([P, PACK], F32, name="us_cols")
+        ident = keep.tile([P, P], F32, name="ident")
+        coef_win = [keep.tile([P, T], F32, name="coef_win%d" % j, tag="coef%d" % j, align_bytes=64) for j in range(E_TILES)]
+
+        nc.vector.memset(scales[:].bitcast(I32), 0)
+        nc.vector.memset(kn_win[0:KN_ROW, :], 0.0)
+        make_identity(nc, ident[:])
+
+        nc.sync.dma_start(offsets[:], offs)
+        nc.sync.dma_start(kn_win[KN_ROW : KN_ROW + 1, :], kn[0:1, :])
+        nc.sync.dma_start(q_raw[:], query.rearrange("(p t) q -> p t q", t=PACK))
+        for r in range(4):
+            nc.sync.dma_start(scales[r:P:32, :].bitcast(I32), pts_scales[0, r:16:4, :].bitcast(I32))
+        nc.sync.dma_start(words[:].bitcast(I32), pts_words[0].rearrange("p n t -> p (n t)").bitcast(I32))
+        with nc.allow_non_contiguous_dma(reason="one number a partition"):
+            nc.sync.dma_start(qn_col[:], qn)
+        nc.sync.dma_start(us_cols[:], us.rearrange("o (s t) -> (o s) t", t=PACK))
+        for j in range(E_TILES):
+            nc.sync.dma_start(coef_win[j][:], coef[P * j : P * (j + 1), :])
+
+        pts_bytes = keep.tile([P, I], U8, name="pts_bytes", align_bytes=64)
+        nc.vector.tensor_copy(pts_bytes[:], scales[:].indirect(offsets[:]))
+        kn_got = keep.tile([P, I], F32, name="kn_got")
+        nc.vector.tensor_copy(kn_got[:], kn_win[:].indirect(offsets[:]))
+        pts_codes = keep.tile([P, I], U32, name="pts_codes", align_bytes=64)
+        nc.vector.tensor_copy(pts_codes[:], words[:].indirect(offsets[:]))
+
+        q_bf = keep.tile([P, Q, PACK], BF16, name="q_bf", align_bytes=64)
+        nc.scalar.activation(q_bf[:], q_raw[:].rearrange("p t q -> p q t"), ACT.Copy)
+        q_codes = keep.tile([P, Q], U32, name="q_codes", align_bytes=64)
+        q_bytes = keep.tile([P, Q], U8, name="q_bytes", align_bytes=64)
+        nc.vector.quantize_mx(out=q_codes[:].bitcast(FP8X4), scales=q_bytes[:], in_=q_bf[:].rearrange("p q t -> p (q t)"))
+
+
+        kn_ps = psum.tile([P, PACK, P], F32, name="kn_ps")
+        for t in range(PACK):
+            nc.tensor.transpose(kn_ps[:, t, :], kn_got[:, t : I : PACK], ident[:])
+        neg_kn = keep.tile([P, PACK], F32, name="neg_kn")
+        nc.scalar.activation(neg_kn[:], kn_ps[:, :, KN_ROW], ACT.Copy, scale=-1.0)
+        a_ps = psum.tile([P, I], F32, name="a_ps")
+        nc.tensor.matmul_mx(
+            out=a_ps[:], lhsT=q_codes[:].bitcast(FP8X4), lhsT_scale=q_bytes[:],
+            rhs=pts_codes[:].bitcast(FP8X4), rhs_scale=pts_bytes[:], start=True, stop=True,
+        )
+        gap = keep.tile([P, PACK, P], F32, name="gap")
+        nc.scalar.activation(gap[:], a_ps[:].rearrange("q (s t) -> q t s", t=PACK), ACT.Identity, bias=qn_col[:], scale=-1.0)
+        gap_ps = psum.tile([P, PACK, Q], F32, name="gap_ps")
+        for t in range(PACK):
+            nc.tensor.transpose(gap_ps[:, t, :], gap[:, t, :], ident[:])
+        gauss = keep.tile([P, PACK, Q], F32, name="gauss")
+        for t in range(PACK):
+            nc.scalar.activation(gauss[:, t, :], gap_ps[:, t, :], ACT.Exp, bias=neg_kn[:, t : t + 1], scale=-1.0)
+
+        def values(j, v_bf):
+            got = keep.tile([P, I], BF16, name="got%d" % j, tag=["words", "kn_win", "got2", "got3"][j])
+            nc.vector.tensor_copy(got[:], coef_win[j][:].indirect(offsets[:]))
+            pairs = got[:].bitcast(F32)
+            v_ps = psum_ring.tile([P, 2, P], F32, name="v_ps")
+            for u in range(2):
+                nc.tensor.transpose(v_ps[:, u, :], pairs[:, u : I // 2 : 2], ident[:])
+            nc.scalar.copy(v_bf.bitcast(F32), v_ps[:].rearrange("s u e -> s e u"))
+            return got
+
+        def product(name, v_bf, width, slot):
+            v_codes = keep.tile([P, width], U32, name="v_codes" + name, tag=slot, align_bytes=64)
+            v_bytes = keep.tile([P, width], U8, name="v_bytes" + name, align_bytes=64)
+            nc.vector.quantize_mx(out=v_codes[:].bitcast(FP8X4), scales=v_bytes[:], in_=v_bf.rearrange("s e t -> s (e t)"))
+            o_ps = psum_ring.tile([P, width], F32, name="o_ps")
+            nc.tensor.matmul_mx(
+                out=o_ps[:], lhsT=w_codes[:].bitcast(FP8X4), lhsT_scale=w_bytes[:],
+                rhs=v_codes[:].bitcast(FP8X4), rhs_scale=v_bytes[:], start=True, stop=True,
+            )
+            return o_ps
+
+        head = keep.tile([P, E - P], F32, name="head")
+        last = keep.tile([P, P], F32, name="last")
+        v_bf01 = keep.tile([P, 2 * P, PACK], BF16, name="v_bf01", align_bytes=64)
+        v_bf2 = keep.tile([P, P, PACK], BF16, name="v_bf2", align_bytes=64)
+        v_bf3 = keep.tile([P, P, PACK], BF16, name="v_bf3", align_bytes=64)
+
+        values(0, v_bf01[:, 0:P, :])
+        w_bf = keep.tile([P, Q, PACK], BF16, name="w_bf", tag="coef0", align_bytes=64)
+        nc.vector.tensor_tensor(
+            w_bf[:], gauss[:].rearrange("s t q -> s q t"), us_cols[:].unsqueeze(1).to_broadcast([P, Q, PACK]), MULT
+        )
+        w_codes = keep.tile([P, Q], U32, name="w_codes", align_bytes=64)
+        w_bytes = keep.tile([P, Q], U8, name="w_bytes", align_bytes=64)
+        nc.vector.quantize_mx(out=w_codes[:].bitcast(FP8X4), scales=w_bytes[:], in_=w_bf[:].rearrange("s q t -> s (q t)"))
+        values(1, v_bf01[:, P : 2 * P, :])
+        values(2, v_bf2[:])
+        nc.scalar.copy(head[:, 0 : 2 * P], product("01", v_bf01[:], 2 * P, "coef2")[:])
+        values(3, v_bf3[:])
+        nc.scalar.copy(head[:, 2 * P : 3 * P], product("2", v_bf2[:], P, "coef3")[:])
+        nc.sync.dma_start(out[:, 0 : E - P], head[:])
+        nc.vector.tensor_copy(last[:], product("3", v_bf3[:], P, "vc3")[:])
+        nc.sync.dma_start(out[:, E - P : E], last[:])

@@ -42,26 +42,26 @@ def tile_attend_kernelridge_kernel(tc, query, pts_words, pts_scales, kn, qn, us,
 
         nc.vector.memset(scales[:].bitcast(I32), 0)
         nc.vector.memset(kn_win[0:KN_ROW, :], 0.0)
+        with nc.allow_non_contiguous_dma(reason="one number a partition"):
+            nc.gpsimd.dma_start(qn_col[:], qn)
+        nc.gpsimd.dma_start(us_cols[:], us.rearrange("o (s t) -> (o s) t", t=PACK))
         make_identity(nc, ident[:])
 
         nc.sync.dma_start(offsets[:], offs)
-        nc.sync.dma_start(kn_win[KN_ROW : KN_ROW + 1, :], kn[0:1, :])
-        nc.sync.dma_start(q_raw[:], query.rearrange("(p t) q -> p t q", t=PACK))
+        nc.scalar.dma_start(kn_win[KN_ROW : KN_ROW + 1, :], kn[0:1, :])
+        nc.sync.dma_start(words[:].bitcast(I32), pts_words[0].rearrange("p n t -> p (n t)").bitcast(I32))
         for r in range(4):
             nc.sync.dma_start(scales[r:P:32, :].bitcast(I32), pts_scales[0, r:16:4, :].bitcast(I32))
-        nc.sync.dma_start(words[:].bitcast(I32), pts_words[0].rearrange("p n t -> p (n t)").bitcast(I32))
-        with nc.allow_non_contiguous_dma(reason="one number a partition"):
-            nc.sync.dma_start(qn_col[:], qn)
-        nc.sync.dma_start(us_cols[:], us.rearrange("o (s t) -> (o s) t", t=PACK))
+        nc.sync.dma_start(q_raw[:], query.rearrange("(p t) q -> p t q", t=PACK))
         for j in range(E_TILES):
             nc.sync.dma_start(coef_win[j][:], coef[P * j : P * (j + 1), :])
 
-        pts_bytes = keep.tile([P, I], U8, name="pts_bytes", align_bytes=64)
-        nc.vector.tensor_copy(pts_bytes[:], scales[:].indirect(offsets[:]))
         kn_got = keep.tile([P, I], F32, name="kn_got")
         nc.vector.tensor_copy(kn_got[:], kn_win[:].indirect(offsets[:]))
         pts_codes = keep.tile([P, I], U32, name="pts_codes", align_bytes=64)
         nc.vector.tensor_copy(pts_codes[:], words[:].indirect(offsets[:]))
+        pts_bytes = keep.tile([P, I], U8, name="pts_bytes", align_bytes=64)
+        nc.vector.tensor_copy(pts_bytes[:], scales[:].indirect(offsets[:]))
 
         q_bf = keep.tile([P, Q, PACK], BF16, name="q_bf", align_bytes=64)
         nc.scalar.activation(q_bf[:], q_raw[:].rearrange("p t q -> p q t"), ACT.Copy)
@@ -90,7 +90,7 @@ def tile_attend_kernelridge_kernel(tc, query, pts_words, pts_scales, kn, qn, us,
             nc.scalar.activation(gauss[:, t, :], gap_ps[:, t, :], ACT.Exp, bias=neg_kn[:, t : t + 1], scale=-1.0)
 
         def values(j, v_bf):
-            got = keep.tile([P, I], BF16, name="got%d" % j, tag=["words", "kn_win", "got2", "got3"][j])
+            got = keep.tile([P, I], BF16, name="got%d" % j, tag=["scales", "words", "got2", "got3"][j])
             nc.vector.tensor_copy(got[:], coef_win[j][:].indirect(offsets[:]))
             pairs = got[:].bitcast(F32)
             v_ps = psum_ring.tile([P, 2, P], F32, name="v_ps")
@@ -117,14 +117,15 @@ def tile_attend_kernelridge_kernel(tc, query, pts_words, pts_scales, kn, qn, us,
         v_bf3 = keep.tile([P, P, PACK], BF16, name="v_bf3", align_bytes=64)
 
         values(0, v_bf01[:, 0:P, :])
-        w_bf = keep.tile([P, Q, PACK], BF16, name="w_bf", tag="coef0", align_bytes=64)
-        nc.vector.tensor_tensor(
-            w_bf[:], gauss[:].rearrange("s t q -> s q t"), us_cols[:].unsqueeze(1).to_broadcast([P, Q, PACK]), MULT
-        )
-        w_codes = keep.tile([P, Q], U32, name="w_codes", align_bytes=64)
+        values(1, v_bf01[:, P : 2 * P, :])
+        w_f32 = keep.tile([P, PACK, Q], F32, name="w_f32")
+        for t in range(PACK):
+            nc.scalar.activation(w_f32[:, t, :], gauss[:, t, :], ACT.Copy, scale=us_cols[:, t : t + 1])
+        w_bf = keep.tile([P, Q, PACK], BF16, name="w_bf", align_bytes=64)
+        nc.scalar.activation(w_bf[:], w_f32[:].rearrange("s t q -> s q t"), ACT.Copy)
+        w_codes = keep.tile([P, Q], U32, name="w_codes", tag="coef1", align_bytes=64)
         w_bytes = keep.tile([P, Q], U8, name="w_bytes", align_bytes=64)
         nc.vector.quantize_mx(out=w_codes[:].bitcast(FP8X4), scales=w_bytes[:], in_=w_bf[:].rearrange("s q t -> s (q t)"))
-        values(1, v_bf01[:, P : 2 * P, :])
         values(2, v_bf2[:])
         nc.scalar.copy(head[:, 0 : 2 * P], product("01", v_bf01[:], 2 * P, "coef2")[:])
         values(3, v_bf3[:])

@@ -42,13 +42,13 @@ def tile_attend_kernelridge_kernel(tc, query, pts_words, pts_scales, kn, qn, us,
 
         nc.vector.memset(scales[:].bitcast(I32), 0)
         nc.vector.memset(kn_win[0:KN_ROW, :], 0.0)
-        with nc.allow_non_contiguous_dma(reason="one number a partition"):
-            nc.gpsimd.dma_start(qn_col[:], qn)
-        nc.gpsimd.dma_start(us_cols[:], us.rearrange("o (s t) -> (o s) t", t=PACK))
         make_identity(nc, ident[:])
 
         nc.sync.dma_start(offsets[:], offs)
-        nc.scalar.dma_start(kn_win[KN_ROW : KN_ROW + 1, :], kn[0:1, :])
+        nc.sync.dma_start(kn_win[KN_ROW : KN_ROW + 1, :], kn[0:1, :])
+        with nc.allow_non_contiguous_dma(reason="one number a partition"):
+            nc.sync.dma_start(qn_col[:], qn)
+        nc.sync.dma_start(us_cols[:], us.rearrange("o (s t) -> (o s) t", t=PACK))
         nc.sync.dma_start(words[:].bitcast(I32), pts_words[0].rearrange("p n t -> p (n t)").bitcast(I32))
         for r in range(4):
             nc.sync.dma_start(scales[r:P:32, :].bitcast(I32), pts_scales[0, r:16:4, :].bitcast(I32))
@@ -99,37 +99,40 @@ def tile_attend_kernelridge_kernel(tc, query, pts_words, pts_scales, kn, qn, us,
             nc.scalar.copy(v_bf.bitcast(F32), v_ps[:].rearrange("s u e -> s e u"))
             return got
 
-        def product(name, v_bf, width, slot):
-            v_codes = keep.tile([P, width], U32, name="v_codes" + name, tag=slot, align_bytes=64)
-            v_bytes = keep.tile([P, width], U8, name="v_bytes" + name, align_bytes=64)
-            nc.vector.quantize_mx(out=v_codes[:].bitcast(FP8X4), scales=v_bytes[:], in_=v_bf.rearrange("s e t -> s (e t)"))
-            o_ps = psum_ring.tile([P, width], F32, name="o_ps")
+        def quantise(name, x_bf, slot):
+            width = x_bf.shape[1]
+            codes = keep.tile([P, width], U32, name="codes_" + name, tag=slot, align_bytes=64)
+            plane = keep.tile([P, width], U8, name="plane_" + name, align_bytes=64)
+            nc.vector.quantize_mx(out=codes[:].bitcast(FP8X4), scales=plane[:], in_=x_bf.rearrange("s c t -> s (c t)"))
+            return codes, plane
+
+        def product(v_codes, v_plane):
+            o_ps = psum_ring.tile([P, v_codes.shape[1]], F32, name="o_ps")
             nc.tensor.matmul_mx(
-                out=o_ps[:], lhsT=w_codes[:].bitcast(FP8X4), lhsT_scale=w_bytes[:],
-                rhs=v_codes[:].bitcast(FP8X4), rhs_scale=v_bytes[:], start=True, stop=True,
+                out=o_ps[:], lhsT=wv_codes[:, 0:Q].bitcast(FP8X4), lhsT_scale=wv_plane[:, 0:Q],
+                rhs=v_codes.bitcast(FP8X4), rhs_scale=v_plane, start=True, stop=True,
             )
             return o_ps
 
         head = keep.tile([P, E - P], F32, name="head")
         last = keep.tile([P, P], F32, name="last")
-        v_bf01 = keep.tile([P, 2 * P, PACK], BF16, name="v_bf01", align_bytes=64)
-        v_bf2 = keep.tile([P, P, PACK], BF16, name="v_bf2", align_bytes=64)
-        v_bf3 = keep.tile([P, P, PACK], BF16, name="v_bf3", align_bytes=64)
+        wv_bf = keep.tile([P, Q + P, PACK], BF16, name="wv_bf", align_bytes=64)
+        mid_bf = keep.tile([P, 2 * P, PACK], BF16, name="mid_bf", align_bytes=64)
+        last_bf = keep.tile([P, P, PACK], BF16, name="last_bf", align_bytes=64)
 
-        values(0, v_bf01[:, 0:P, :])
-        values(1, v_bf01[:, P : 2 * P, :])
+        values(0, wv_bf[:, Q : Q + P, :])
         w_f32 = keep.tile([P, PACK, Q], F32, name="w_f32")
         for t in range(PACK):
             nc.scalar.activation(w_f32[:, t, :], gauss[:, t, :], ACT.Copy, scale=us_cols[:, t : t + 1])
-        w_bf = keep.tile([P, Q, PACK], BF16, name="w_bf", align_bytes=64)
-        nc.scalar.activation(w_bf[:], w_f32[:].rearrange("s t q -> s q t"), ACT.Copy)
-        w_codes = keep.tile([P, Q], U32, name="w_codes", tag="coef1", align_bytes=64)
-        w_bytes = keep.tile([P, Q], U8, name="w_bytes", align_bytes=64)
-        nc.vector.quantize_mx(out=w_codes[:].bitcast(FP8X4), scales=w_bytes[:], in_=w_bf[:].rearrange("s q t -> s (q t)"))
-        values(2, v_bf2[:])
-        nc.scalar.copy(head[:, 0 : 2 * P], product("01", v_bf01[:], 2 * P, "coef2")[:])
-        values(3, v_bf3[:])
-        nc.scalar.copy(head[:, 2 * P : 3 * P], product("2", v_bf2[:], P, "coef3")[:])
+        nc.scalar.activation(wv_bf[:, 0:Q, :], w_f32[:].rearrange("s t q -> s q t"), ACT.Copy)
+        values(1, mid_bf[:, 0:P, :])
+        values(2, mid_bf[:, P : 2 * P, :])
+        wv_codes, wv_plane = quantise("wv", wv_bf[:], "coef2")
+        nc.scalar.copy(head[:, 0:P], product(wv_codes[:, Q : Q + P], wv_plane[:, Q : Q + P])[:])
+        values(3, last_bf[:])
+        mid_codes, mid_plane = quantise("mid", mid_bf[:], "coef3")
+        nc.scalar.copy(head[:, P : 3 * P], product(mid_codes[:], mid_plane[:])[:])
         nc.sync.dma_start(out[:, 0 : E - P], head[:])
-        nc.vector.tensor_copy(last[:], product("3", v_bf3[:], P, "vc3")[:])
+        last_codes, last_plane = quantise("last", last_bf[:], "last_codes")
+        nc.vector.tensor_copy(last[:], product(last_codes[:], last_plane[:])[:])
         nc.sync.dma_start(out[:, E - P : E], last[:])

@@ -28,6 +28,7 @@ def tile_attend_kernelridge_kernel(tc, query, pts_words, pts_scales, kn, qn, us,
     with ExitStack() as ctx:
         keep = ctx.enter_context(tc.tile_pool(name="keep", bufs=1))
         psum = ctx.enter_context(tc.psum_pool(name="psum", bufs=1))
+        psum_out = ctx.enter_context(tc.psum_pool(name="psum_out", bufs=3))
         psum_ring = ctx.enter_context(tc.psum_pool(name="psum_ring", bufs=2))
 
         offsets = keep.tile([P, I // 16], U16, name="offsets")
@@ -48,8 +49,8 @@ def tile_attend_kernelridge_kernel(tc, query, pts_words, pts_scales, kn, qn, us,
         nc.sync.dma_start(kn_win[KN_ROW : KN_ROW + 1, :], kn[0:1, :])
         with nc.allow_non_contiguous_dma(reason="one number a partition"):
             nc.sync.dma_start(qn_col[:], qn)
-        nc.sync.dma_start(us_cols[:], us.rearrange("o (s t) -> (o s) t", t=PACK))
         nc.sync.dma_start(words[:].bitcast(I32), pts_words[0].rearrange("p n t -> p (n t)").bitcast(I32))
+        nc.sync.dma_start(us_cols[:], us.rearrange("o (s t) -> (o s) t", t=PACK))
         for r in range(4):
             nc.sync.dma_start(scales[r:P:32, :].bitcast(I32), pts_scales[0, r:16:4, :].bitcast(I32))
         nc.sync.dma_start(q_raw[:], query.rearrange("(p t) q -> p t q", t=PACK))
@@ -107,32 +108,34 @@ def tile_attend_kernelridge_kernel(tc, query, pts_words, pts_scales, kn, qn, us,
             return codes, plane
 
         def product(v_codes, v_plane):
-            o_ps = psum_ring.tile([P, v_codes.shape[1]], F32, name="o_ps")
+            o_ps = psum_out.tile([P, v_codes.shape[1]], F32, name="o_ps")
             nc.tensor.matmul_mx(
                 out=o_ps[:], lhsT=wv_codes[:, 0:Q].bitcast(FP8X4), lhsT_scale=wv_plane[:, 0:Q],
                 rhs=v_codes.bitcast(FP8X4), rhs_scale=v_plane, start=True, stop=True,
             )
             return o_ps
 
-        head = keep.tile([P, E - P], F32, name="head")
-        last = keep.tile([P, P], F32, name="last")
+        head_bf = keep.tile([P, 2 * P, PACK], BF16, name="head_bf", align_bytes=64)
         wv_bf = keep.tile([P, Q + P, PACK], BF16, name="wv_bf", align_bytes=64)
-        mid_bf = keep.tile([P, 2 * P, PACK], BF16, name="mid_bf", align_bytes=64)
         last_bf = keep.tile([P, P, PACK], BF16, name="last_bf", align_bytes=64)
 
-        values(0, wv_bf[:, Q : Q + P, :])
+        values(0, head_bf[:, 0:P, :])
         w_f32 = keep.tile([P, PACK, Q], F32, name="w_f32")
         for t in range(PACK):
             nc.scalar.activation(w_f32[:, t, :], gauss[:, t, :], ACT.Copy, scale=us_cols[:, t : t + 1])
         nc.scalar.activation(wv_bf[:, 0:Q, :], w_f32[:].rearrange("s t q -> s q t"), ACT.Copy)
-        values(1, mid_bf[:, 0:P, :])
-        values(2, mid_bf[:, P : 2 * P, :])
-        wv_codes, wv_plane = quantise("wv", wv_bf[:], "coef2")
-        nc.scalar.copy(head[:, 0:P], product(wv_codes[:, Q : Q + P], wv_plane[:, Q : Q + P])[:])
+        values(1, head_bf[:, P : 2 * P, :])
+        values(2, wv_bf[:, Q : Q + P, :])
+        head_codes, head_plane = quantise("head", head_bf[:], "coef2")
         values(3, last_bf[:])
-        mid_codes, mid_plane = quantise("mid", mid_bf[:], "coef3")
-        nc.scalar.copy(head[:, P : 3 * P], product(mid_codes[:], mid_plane[:])[:])
-        nc.sync.dma_start(out[:, 0 : E - P], head[:])
+        wv_codes, wv_plane = quantise("wv", wv_bf[:], "coef3")
+        head = keep.tile([P, 2 * P], F32, name="head")
+        nc.scalar.copy(head[:], product(head_codes[:], head_plane[:])[:])
+        nc.sync.dma_start(out[:, 0 : 2 * P], head[:])
+        mid = keep.tile([P, P], F32, name="mid")
+        nc.scalar.copy(mid[:], product(wv_codes[:, Q : Q + P], wv_plane[:, Q : Q + P])[:])
+        nc.sync.dma_start(out[:, 2 * P : 3 * P], mid[:])
         last_codes, last_plane = quantise("last", last_bf[:], "last_codes")
+        last = keep.tile([P, P], F32, name="last")
         nc.vector.tensor_copy(last[:], product(last_codes[:], last_plane[:])[:])
         nc.sync.dma_start(out[:, E - P : E], last[:])

@@ -20,6 +20,8 @@ MULT = mybir.AluOpType.mult
 P = 128
 PACK = 4
 KN_ROW = P - 1
+SCALE_ROWS = 16
+SCALE_ROW0 = 48
 E_TILES = E // P
 
 
@@ -32,40 +34,53 @@ def tile_attend_kernelridge_kernel(tc, query, pts_words, pts_scales, kn, qn, us,
         psum_ring = ctx.enter_context(tc.psum_pool(name="psum_ring", bufs=2))
 
         offsets = keep.tile([P, I // 16], U16, name="offsets")
-        words = keep.tile([P, T], U32, name="words", tag="words")
+        words = keep.tile([P, T], U32, name="words", tag="coef2", align_bytes=64)
         scales = keep.tile([P, T], U8, name="scales", tag="scales")
-        kn_win = keep.tile([P, T], F32, name="kn_win", tag="kn_win")
-        q_raw = keep.tile([P, PACK, Q], F32, name="q_raw")
+        kn_win = keep.tile([P, T], F32, name="kn_win", tag="coef1", align_bytes=64)
+        pts_plane = keep.tile([P, I], U8, name="pts_plane", align_bytes=64)
+        q_raw = keep.tile([P, PACK, Q], F32, name="q_raw", tag="coef3", align_bytes=64)
         qn_col = keep.tile([P, 1], F32, name="qn_col")
         us_cols = keep.tile([P, PACK], F32, name="us_cols")
         ident = keep.tile([P, P], F32, name="ident")
-        coef_win = [keep.tile([P, T], F32, name="coef_win%d" % j, tag="coef%d" % j, align_bytes=64) for j in range(E_TILES)]
 
-        nc.vector.memset(scales[:].bitcast(I32), 0)
+        def load_coef(j):
+            win = keep.tile([P, T], F32, name="coef_win%d" % j, tag="coef%d" % j, align_bytes=64)
+            nc.sync.dma_start(win[:], coef[P * j : P * (j + 1), :])
+            return win
+
+        nc.gpsimd.memset(scales[0:SCALE_ROW0, :].bitcast(I32), 0)
+        nc.gpsimd.memset(scales[SCALE_ROW0 + SCALE_ROWS : P, :].bitcast(I32), 0)
+        nc.gpsimd.memset(pts_plane[:].bitcast(I32), 0)
         nc.vector.memset(kn_win[0:KN_ROW, :], 0.0)
         make_identity(nc, ident[:])
 
         nc.sync.dma_start(offsets[:], offs)
-        nc.sync.dma_start(kn_win[KN_ROW : KN_ROW + 1, :], kn[0:1, :])
+        nc.scalar.dma_start(kn_win[KN_ROW : KN_ROW + 1, :], kn[0:1, :])
+        nc.sync.dma_start(scales[SCALE_ROW0 : SCALE_ROW0 + SCALE_ROWS, :].bitcast(I32), pts_scales[0].bitcast(I32))
         with nc.allow_non_contiguous_dma(reason="one number a partition"):
-            nc.sync.dma_start(qn_col[:], qn)
+            nc.scalar.dma_start(qn_col[:], qn)
         nc.sync.dma_start(words[:].bitcast(I32), pts_words[0].rearrange("p n t -> p (n t)").bitcast(I32))
-        nc.sync.dma_start(us_cols[:], us.rearrange("o (s t) -> (o s) t", t=PACK))
-        for r in range(4):
-            nc.sync.dma_start(scales[r:P:32, :].bitcast(I32), pts_scales[0, r:16:4, :].bitcast(I32))
+        nc.scalar.dma_start(us_cols[:], us.rearrange("o (s t) -> (o s) t", t=PACK))
         nc.sync.dma_start(q_raw[:], query.rearrange("(p t) q -> p t q", t=PACK))
-        for j in range(E_TILES):
-            nc.sync.dma_start(coef_win[j][:], coef[P * j : P * (j + 1), :])
+        coef_win = [load_coef(0)]
 
-        kn_got = keep.tile([P, I], F32, name="kn_got")
+        scale_got = keep.tile([P, I], U8, name="scale_got", align_bytes=64)
+        nc.vector.tensor_copy(scale_got[:], scales[:].indirect(offsets[:]))
+        for r in range(4):
+            nc.sync.dma_start(
+                pts_plane[r:P:32, :].bitcast(I32),
+                scale_got[SCALE_ROW0 + r : SCALE_ROW0 + SCALE_ROWS : 4, :].bitcast(I32),
+            )
+        kn_got = keep.tile([P, I], F32, name="kn_got", tag="scales")
         nc.vector.tensor_copy(kn_got[:], kn_win[:].indirect(offsets[:]))
+        coef_win.append(load_coef(1))
         pts_codes = keep.tile([P, I], U32, name="pts_codes", align_bytes=64)
         nc.vector.tensor_copy(pts_codes[:], words[:].indirect(offsets[:]))
-        pts_bytes = keep.tile([P, I], U8, name="pts_bytes", align_bytes=64)
-        nc.vector.tensor_copy(pts_bytes[:], scales[:].indirect(offsets[:]))
+        coef_win.append(load_coef(2))
 
         q_bf = keep.tile([P, Q, PACK], BF16, name="q_bf", align_bytes=64)
         nc.scalar.activation(q_bf[:], q_raw[:].rearrange("p t q -> p q t"), ACT.Copy)
+        coef_win.append(load_coef(3))
         q_codes = keep.tile([P, Q], U32, name="q_codes", align_bytes=64)
         q_bytes = keep.tile([P, Q], U8, name="q_bytes", align_bytes=64)
         nc.vector.quantize_mx(out=q_codes[:].bitcast(FP8X4), scales=q_bytes[:], in_=q_bf[:].rearrange("p q t -> p (q t)"))
@@ -79,11 +94,11 @@ def tile_attend_kernelridge_kernel(tc, query, pts_words, pts_scales, kn, qn, us,
         a_ps = psum.tile([P, I], F32, name="a_ps")
         nc.tensor.matmul_mx(
             out=a_ps[:], lhsT=q_codes[:].bitcast(FP8X4), lhsT_scale=q_bytes[:],
-            rhs=pts_codes[:].bitcast(FP8X4), rhs_scale=pts_bytes[:], start=True, stop=True,
+            rhs=pts_codes[:].bitcast(FP8X4), rhs_scale=pts_plane[:], start=True, stop=True,
         )
         gap = keep.tile([P, PACK, P], F32, name="gap")
         nc.scalar.activation(gap[:], a_ps[:].rearrange("q (s t) -> q t s", t=PACK), ACT.Identity, bias=qn_col[:], scale=-1.0)
-        gap_ps = psum.tile([P, PACK, Q], F32, name="gap_ps")
+        gap_ps = psum.tile([P, PACK, Q], F32, name="gap_ps", tag="gap_ps")
         for t in range(PACK):
             nc.tensor.transpose(gap_ps[:, t, :], gap[:, t, :], ident[:])
         gauss = keep.tile([P, PACK, Q], F32, name="gauss")
@@ -91,10 +106,13 @@ def tile_attend_kernelridge_kernel(tc, query, pts_words, pts_scales, kn, qn, us,
             nc.scalar.activation(gauss[:, t, :], gap_ps[:, t, :], ACT.Exp, bias=neg_kn[:, t : t + 1], scale=-1.0)
 
         def values(j, v_bf):
-            got = keep.tile([P, I], BF16, name="got%d" % j, tag=["scales", "words", "got2", "got3"][j])
+            got = keep.tile([P, I], BF16, name="got%d" % j)
             nc.vector.tensor_copy(got[:], coef_win[j][:].indirect(offsets[:]))
             pairs = got[:].bitcast(F32)
-            v_ps = psum_ring.tile([P, 2, P], F32, name="v_ps")
+            if j == 0:
+                v_ps = psum.tile([P, 2, P], F32, name="v_ps0", tag="gap_ps")
+            else:
+                v_ps = psum_ring.tile([P, 2, P], F32, name="v_ps")
             for u in range(2):
                 nc.tensor.transpose(v_ps[:, u, :], pairs[:, u : I // 2 : 2], ident[:])
             nc.scalar.copy(v_bf.bitcast(F32), v_ps[:].rearrange("s u e -> s e u"))
@@ -115,26 +133,26 @@ def tile_attend_kernelridge_kernel(tc, query, pts_words, pts_scales, kn, qn, us,
             )
             return o_ps
 
-        head_bf = keep.tile([P, 2 * P, PACK], BF16, name="head_bf", align_bytes=64)
         wv_bf = keep.tile([P, Q + P, PACK], BF16, name="wv_bf", align_bytes=64)
+        mid_bf = keep.tile([P, 2 * P, PACK], BF16, name="mid_bf", align_bytes=64)
         last_bf = keep.tile([P, P, PACK], BF16, name="last_bf", align_bytes=64)
 
-        values(0, head_bf[:, 0:P, :])
-        w_f32 = keep.tile([P, PACK, Q], F32, name="w_f32")
-        for t in range(PACK):
-            nc.scalar.activation(w_f32[:, t, :], gauss[:, t, :], ACT.Copy, scale=us_cols[:, t : t + 1])
-        nc.scalar.activation(wv_bf[:, 0:Q, :], w_f32[:].rearrange("s t q -> s q t"), ACT.Copy)
-        values(1, head_bf[:, P : 2 * P, :])
-        values(2, wv_bf[:, Q : Q + P, :])
-        head_codes, head_plane = quantise("head", head_bf[:], "coef2")
+        values(0, wv_bf[:, Q : Q + P, :])
+        nc.vector.tensor_tensor(
+            wv_bf[:, 0:Q, :], gauss[:].rearrange("s t q -> s q t"),
+            us_cols[:].unsqueeze(1).to_broadcast([P, Q, PACK]), MULT,
+        )
+        values(1, mid_bf[:, 0:P, :])
+        values(2, mid_bf[:, P : 2 * P, :])
+        wv_codes, wv_plane = quantise("wv", wv_bf[:], "coef2")
+        head = keep.tile([P, P], F32, name="head")
+        nc.scalar.copy(head[:], product(wv_codes[:, Q : Q + P], wv_plane[:, Q : Q + P])[:])
+        nc.sync.dma_start(out[:, 0:P], head[:])
         values(3, last_bf[:])
-        wv_codes, wv_plane = quantise("wv", wv_bf[:], "coef3")
-        head = keep.tile([P, 2 * P], F32, name="head")
-        nc.scalar.copy(head[:], product(head_codes[:], head_plane[:])[:])
-        nc.sync.dma_start(out[:, 0 : 2 * P], head[:])
-        mid = keep.tile([P, P], F32, name="mid")
-        nc.scalar.copy(mid[:], product(wv_codes[:, Q : Q + P], wv_plane[:, Q : Q + P])[:])
-        nc.sync.dma_start(out[:, 2 * P : 3 * P], mid[:])
+        mid_codes, mid_plane = quantise("mid", mid_bf[:], "coef3")
+        mid = keep.tile([P, 2 * P], F32, name="mid")
+        nc.scalar.copy(mid[:], product(mid_codes[:], mid_plane[:])[:])
+        nc.sync.dma_start(out[:, P : 3 * P], mid[:])
         last_codes, last_plane = quantise("last", last_bf[:], "last_codes")
         last = keep.tile([P, P], F32, name="last")
         nc.vector.tensor_copy(last[:], product(last_codes[:], last_plane[:])[:])

@@ -86,7 +86,7 @@ def tile_attend_kernelridge_kernel(tc, query, pts_words, pts_scales, kn, qn, us,
         nc.vector.quantize_mx(out=q_codes[:].bitcast(FP8X4), scales=q_bytes[:], in_=q_bf[:].rearrange("p q t -> p (q t)"))
 
 
-        kn_ps = psum.tile([P, PACK, P], F32, name="kn_ps")
+        kn_ps = psum.tile([P, PACK, P], F32, name="kn_ps", tag="kn_ps")
         for t in range(PACK):
             nc.tensor.transpose(kn_ps[:, t, :], kn_got[:, t : I : PACK], ident[:])
         neg_kn = keep.tile([P, PACK], F32, name="neg_kn")
@@ -96,33 +96,44 @@ def tile_attend_kernelridge_kernel(tc, query, pts_words, pts_scales, kn, qn, us,
             out=a_ps[:], lhsT=q_codes[:].bitcast(FP8X4), lhsT_scale=q_bytes[:],
             rhs=pts_codes[:].bitcast(FP8X4), rhs_scale=pts_plane[:], start=True, stop=True,
         )
-        gap = keep.tile([P, PACK, P], F32, name="gap")
-        nc.scalar.activation(gap[:], a_ps[:].rearrange("q (s t) -> q t s", t=PACK), ACT.Identity, bias=qn_col[:], scale=-1.0)
-        gap_ps = psum.tile([P, PACK, Q], F32, name="gap_ps", tag="gap_ps")
+        gap = [keep.tile([P, 2, P], F32, name="gap%d" % h) for h in range(2)]
+        dealt = a_ps[:].rearrange("q (s t) -> q t s", t=PACK)
+        for h in range(2):
+            nc.scalar.activation(gap[h][:], dealt[:, 2 * h : 2 * h + 2, :], ACT.Identity, bias=qn_col[:], scale=-1.0)
+        gap_ps = [psum.tile([P, 2, Q], F32, name="gap_ps%d" % h, tag=["gap_ps", "kn_ps"][h]) for h in range(2)]
         for t in range(PACK):
-            nc.tensor.transpose(gap_ps[:, t, :], gap[:, t, :], ident[:])
+            nc.tensor.transpose(gap_ps[t // 2][:, t % 2, :], gap[t // 2][:, t % 2, :], ident[:])
         gauss = keep.tile([P, PACK, Q], F32, name="gauss")
         for t in range(PACK):
-            nc.scalar.activation(gauss[:, t, :], gap_ps[:, t, :], ACT.Exp, bias=neg_kn[:, t : t + 1], scale=-1.0)
+            nc.scalar.activation(gauss[:, t, :], gap_ps[t // 2][:, t % 2, :], ACT.Exp, bias=neg_kn[:, t : t + 1], scale=-1.0)
 
-        def values(j, v_bf):
+        def gather(j):
             got = keep.tile([P, I], BF16, name="got%d" % j)
             nc.vector.tensor_copy(got[:], coef_win[j][:].indirect(offsets[:]))
+            return got
+
+        def values(j, v_bf):
+            turn(j, gather(j), v_bf)
+
+        def turn(j, got, v_bf):
             pairs = got[:].bitcast(F32)
             if j == 0:
-                v_ps = psum.tile([P, 2, P], F32, name="v_ps0", tag="gap_ps")
+                v_ps = psum.tile([P, 2, P], F32, name="v_ps0", tag="kn_ps")
             else:
                 v_ps = psum_ring.tile([P, 2, P], F32, name="v_ps")
             for u in range(2):
                 nc.tensor.transpose(v_ps[:, u, :], pairs[:, u : I // 2 : 2], ident[:])
             nc.scalar.copy(v_bf.bitcast(F32), v_ps[:].rearrange("s u e -> s e u"))
-            return got
 
-        def quantise(name, x_bf, slot):
+        def quantise(name, x_bf, slot, cuts):
             width = x_bf.shape[1]
             codes = keep.tile([P, width], U32, name="codes_" + name, tag=slot, align_bytes=64)
             plane = keep.tile([P, width], U8, name="plane_" + name, align_bytes=64)
-            nc.vector.quantize_mx(out=codes[:].bitcast(FP8X4), scales=plane[:], in_=x_bf.rearrange("s c t -> s (c t)"))
+            for lo, hi in cuts:
+                nc.vector.quantize_mx(
+                    out=codes[:, lo:hi].bitcast(FP8X4), scales=plane[:, lo:hi],
+                    in_=x_bf[:, lo:hi, :].rearrange("s c t -> s (c t)"),
+                )
             return codes, plane
 
         def product(v_codes, v_plane):
@@ -133,27 +144,29 @@ def tile_attend_kernelridge_kernel(tc, query, pts_words, pts_scales, kn, qn, us,
             )
             return o_ps
 
-        wv_bf = keep.tile([P, Q + P, PACK], BF16, name="wv_bf", align_bytes=64)
-        mid_bf = keep.tile([P, 2 * P, PACK], BF16, name="mid_bf", align_bytes=64)
+        mid_bf = keep.tile([P, P, PACK], BF16, name="mid_bf", align_bytes=64)
         last_bf = keep.tile([P, P, PACK], BF16, name="last_bf", align_bytes=64)
 
-        values(0, wv_bf[:, Q : Q + P, :])
+        got0 = gather(0)
+        got1 = gather(1)
+        wv_bf = keep.tile([P, Q + 2 * P, PACK], BF16, name="wv_bf", tag="coef1", align_bytes=64)
+        turn(0, got0, wv_bf[:, Q : Q + P, :])
         nc.vector.tensor_tensor(
-            wv_bf[:, 0:Q, :], gauss[:].rearrange("s t q -> s q t"),
-            us_cols[:].unsqueeze(1).to_broadcast([P, Q, PACK]), MULT,
+            wv_bf[:, 0:Q, :].rearrange("s (c i) t -> s c t i", i=4), gauss[:].rearrange("s t (c i) -> s c t i", i=4),
+            us_cols[:].unsqueeze(1).unsqueeze(3).to_broadcast([P, Q // 4, PACK, 4]), MULT,
         )
-        values(1, mid_bf[:, 0:P, :])
-        values(2, mid_bf[:, P : 2 * P, :])
-        wv_codes, wv_plane = quantise("wv", wv_bf[:], "coef2")
-        head = keep.tile([P, P], F32, name="head")
-        nc.scalar.copy(head[:], product(wv_codes[:, Q : Q + P], wv_plane[:, Q : Q + P])[:])
-        nc.sync.dma_start(out[:, 0:P], head[:])
+        turn(1, got1, wv_bf[:, Q + P : Q + 2 * P, :])
+        values(2, mid_bf[:])
+        wv_codes, wv_plane = quantise("wv", wv_bf[:], "coef2", [(0, Q + P), (Q + P, Q + 2 * P)])
+        head = keep.tile([P, 2 * P], F32, name="head")
+        nc.scalar.copy(head[:], product(wv_codes[:, Q : Q + 2 * P], wv_plane[:, Q : Q + 2 * P])[:])
+        nc.sync.dma_start(out[:, 0 : 2 * P], head[:])
         values(3, last_bf[:])
-        mid_codes, mid_plane = quantise("mid", mid_bf[:], "coef3")
-        mid = keep.tile([P, 2 * P], F32, name="mid")
+        mid_codes, mid_plane = quantise("mid", mid_bf[:], "coef3", [(0, P)])
+        mid = keep.tile([P, P], F32, name="mid")
         nc.scalar.copy(mid[:], product(mid_codes[:], mid_plane[:])[:])
-        nc.sync.dma_start(out[:, P : 3 * P], mid[:])
-        last_codes, last_plane = quantise("last", last_bf[:], "last_codes")
+        nc.sync.dma_start(out[:, 2 * P : 3 * P], mid[:])
+        last_codes, last_plane = quantise("last", last_bf[:], "last_codes", [(0, P)])
         last = keep.tile([P, P], F32, name="last")
         nc.vector.tensor_copy(last[:], product(last_codes[:], last_plane[:])[:])
         nc.sync.dma_start(out[:, E - P : E], last[:])

@@ -34,11 +34,11 @@ def tile_attend_kernelridge_kernel(tc, query, pts_words, pts_scales, kn, qn, us,
         psum_ring = ctx.enter_context(tc.psum_pool(name="psum_ring", bufs=2))
 
         offsets = keep.tile([P, I // 16], U16, name="offsets")
-        words = keep.tile([P, T], U32, name="words", tag="coef2", align_bytes=64)
-        scales = keep.tile([P, T], U8, name="scales", tag="scales")
-        kn_win = keep.tile([P, T], F32, name="kn_win", tag="coef1", align_bytes=64)
+        words = keep.tile([P, T], U32, name="words", tag="coef3", align_bytes=64)
+        scales = keep.tile([P, T], U8, name="scales", tag="coef1", align_bytes=64)
+        kn_win = keep.tile([P, T], F32, name="kn_win", tag="kn_win", align_bytes=64)
         pts_plane = keep.tile([P, I], U8, name="pts_plane", align_bytes=64)
-        q_raw = keep.tile([P, PACK, Q], F32, name="q_raw", tag="coef3", align_bytes=64)
+        q_raw = keep.tile([P, PACK, Q], F32, name="q_raw", tag="coef2", align_bytes=64)
         qn_col = keep.tile([P, 1], F32, name="qn_col")
         us_cols = keep.tile([P, PACK], F32, name="us_cols")
         ident = keep.tile([P, P], F32, name="ident")
@@ -51,17 +51,17 @@ def tile_attend_kernelridge_kernel(tc, query, pts_words, pts_scales, kn, qn, us,
         nc.gpsimd.memset(scales[0:SCALE_ROW0, :].bitcast(I32), 0)
         nc.gpsimd.memset(scales[SCALE_ROW0 + SCALE_ROWS : P, :].bitcast(I32), 0)
         nc.gpsimd.memset(pts_plane[:].bitcast(I32), 0)
-        nc.vector.memset(kn_win[0:KN_ROW, :], 0.0)
+        nc.gpsimd.memset(kn_win[0:KN_ROW, :], 0.0)
         make_identity(nc, ident[:])
 
         nc.sync.dma_start(offsets[:], offs)
-        nc.scalar.dma_start(kn_win[KN_ROW : KN_ROW + 1, :], kn[0:1, :])
+        nc.scalar.dma_start(q_raw[:], query.rearrange("(p t) q -> p t q", t=PACK))
         nc.sync.dma_start(scales[SCALE_ROW0 : SCALE_ROW0 + SCALE_ROWS, :].bitcast(I32), pts_scales[0].bitcast(I32))
+        nc.sync.dma_start(kn_win[KN_ROW : KN_ROW + 1, :], kn[0:1, :])
         with nc.allow_non_contiguous_dma(reason="one number a partition"):
             nc.scalar.dma_start(qn_col[:], qn)
         nc.sync.dma_start(words[:].bitcast(I32), pts_words[0].rearrange("p n t -> p (n t)").bitcast(I32))
         nc.scalar.dma_start(us_cols[:], us.rearrange("o (s t) -> (o s) t", t=PACK))
-        nc.sync.dma_start(q_raw[:], query.rearrange("(p t) q -> p t q", t=PACK))
         coef_win = [load_coef(0)]
 
         scale_got = keep.tile([P, I], U8, name="scale_got", align_bytes=64)
@@ -71,17 +71,17 @@ def tile_attend_kernelridge_kernel(tc, query, pts_words, pts_scales, kn, qn, us,
                 pts_plane[r:P:32, :].bitcast(I32),
                 scale_got[SCALE_ROW0 + r : SCALE_ROW0 + SCALE_ROWS : 4, :].bitcast(I32),
             )
-        kn_got = keep.tile([P, I], F32, name="kn_got", tag="scales")
-        nc.vector.tensor_copy(kn_got[:], kn_win[:].indirect(offsets[:]))
         coef_win.append(load_coef(1))
+        kn_got = keep.tile([P, I], F32, name="kn_got")
+        nc.vector.tensor_copy(kn_got[:], kn_win[:].indirect(offsets[:]))
         pts_codes = keep.tile([P, I], U32, name="pts_codes", align_bytes=64)
         nc.vector.tensor_copy(pts_codes[:], words[:].indirect(offsets[:]))
-        coef_win.append(load_coef(2))
 
         q_bf = keep.tile([P, Q, PACK], BF16, name="q_bf", align_bytes=64)
         nc.scalar.activation(q_bf[:], q_raw[:].rearrange("p t q -> p q t"), ACT.Copy)
+        coef_win.append(load_coef(2))
         coef_win.append(load_coef(3))
-        q_codes = keep.tile([P, Q], U32, name="q_codes", align_bytes=64)
+        q_codes = keep.tile([P, Q], U32, name="q_codes", tag="kn_win", align_bytes=64)
         q_bytes = keep.tile([P, Q], U8, name="q_bytes", align_bytes=64)
         nc.vector.quantize_mx(out=q_codes[:].bitcast(FP8X4), scales=q_bytes[:], in_=q_bf[:].rearrange("p q t -> p (q t)"))
 
@@ -150,11 +150,11 @@ def tile_attend_kernelridge_kernel(tc, query, pts_words, pts_scales, kn, qn, us,
         got0 = gather(0)
         got1 = gather(1)
         wv_bf = keep.tile([P, Q + 2 * P, PACK], BF16, name="wv_bf", tag="coef1", align_bytes=64)
-        turn(0, got0, wv_bf[:, Q : Q + P, :])
         nc.vector.tensor_tensor(
             wv_bf[:, 0:Q, :].rearrange("s (c i) t -> s c t i", i=4), gauss[:].rearrange("s t (c i) -> s c t i", i=4),
             us_cols[:].unsqueeze(1).unsqueeze(3).to_broadcast([P, Q // 4, PACK, 4]), MULT,
         )
+        turn(0, got0, wv_bf[:, Q : Q + P, :])
         turn(1, got1, wv_bf[:, Q + P : Q + 2 * P, :])
         values(2, mid_bf[:])
         wv_codes, wv_plane = quantise("wv", wv_bf[:], "coef2", [(0, Q + P), (Q + P, Q + 2 * P)])

@@ -39,8 +39,8 @@ def tile_attend_kernelridge_kernel(tc, query, pts_words, pts_scales, kn, qn, us,
         kn_win = keep.tile([P, T], F32, name="kn_win", tag="kn_win", align_bytes=64)
         pts_plane = keep.tile([P, I], U8, name="pts_plane", align_bytes=64)
         q_raw = keep.tile([P, PACK, Q], F32, name="q_raw", tag="coef2", align_bytes=64)
-        qn_col = keep.tile([P, 1], F32, name="qn_col")
-        us_cols = keep.tile([P, PACK], F32, name="us_cols")
+        us_row = keep.tile([P, I], F32, name="us_row")
+        qn_row = keep.tile([P, Q], F32, name="qn_row")
         ident = keep.tile([P, P], F32, name="ident")
 
         def load_coef(j):
@@ -51,17 +51,18 @@ def tile_attend_kernelridge_kernel(tc, query, pts_words, pts_scales, kn, qn, us,
         nc.gpsimd.memset(scales[0:SCALE_ROW0, :].bitcast(I32), 0)
         nc.gpsimd.memset(scales[SCALE_ROW0 + SCALE_ROWS : P, :].bitcast(I32), 0)
         nc.gpsimd.memset(pts_plane[:].bitcast(I32), 0)
-        nc.gpsimd.memset(kn_win[0:KN_ROW, :], 0.0)
+        nc.vector.memset(kn_win[0:KN_ROW, :], 0.0)
         make_identity(nc, ident[:])
+        nc.gpsimd.memset(qn_row[0:KN_ROW, :], 0.0)
+        nc.gpsimd.memset(us_row[0:KN_ROW, :], 0.0)
 
+        nc.sync.dma_start(q_raw[:], query.rearrange("(p t) q -> p t q", t=PACK))
+        nc.scalar.dma_start(kn_win[KN_ROW : KN_ROW + 1, :], kn[0:1, :])
         nc.sync.dma_start(offsets[:], offs)
-        nc.scalar.dma_start(q_raw[:], query.rearrange("(p t) q -> p t q", t=PACK))
         nc.sync.dma_start(scales[SCALE_ROW0 : SCALE_ROW0 + SCALE_ROWS, :].bitcast(I32), pts_scales[0].bitcast(I32))
-        nc.sync.dma_start(kn_win[KN_ROW : KN_ROW + 1, :], kn[0:1, :])
-        with nc.allow_non_contiguous_dma(reason="one number a partition"):
-            nc.scalar.dma_start(qn_col[:], qn)
+        nc.scalar.dma_start(qn_row[KN_ROW : KN_ROW + 1, :], qn.rearrange("q o -> o q"))
         nc.sync.dma_start(words[:].bitcast(I32), pts_words[0].rearrange("p n t -> p (n t)").bitcast(I32))
-        nc.scalar.dma_start(us_cols[:], us.rearrange("o (s t) -> (o s) t", t=PACK))
+        nc.scalar.dma_start(us_row[KN_ROW : KN_ROW + 1, :], us)
         coef_win = [load_coef(0)]
 
         scale_got = keep.tile([P, I], U8, name="scale_got", align_bytes=64)
@@ -86,12 +87,21 @@ def tile_attend_kernelridge_kernel(tc, query, pts_words, pts_scales, kn, qn, us,
         nc.vector.quantize_mx(out=q_codes[:].bitcast(FP8X4), scales=q_bytes[:], in_=q_bf[:].rearrange("p q t -> p (q t)"))
 
 
+        qn_ps = psum.tile([P, P], F32, name="qn_ps", tag="a_ps")
+        nc.tensor.transpose(qn_ps[:], qn_row[:], ident[:])
+        qn_col = keep.tile([P, 1], F32, name="qn_col")
+        nc.scalar.copy(qn_col[:], qn_ps[:, KN_ROW : KN_ROW + 1])
+        us_ps = psum.tile([P, PACK, P], F32, name="us_ps", tag="gap_ps")
+        for t in range(PACK):
+            nc.tensor.transpose(us_ps[:, t, :], us_row[:, t : I : PACK], ident[:])
+        us_cols = keep.tile([P, PACK], F32, name="us_cols")
+        nc.scalar.copy(us_cols[:], us_ps[:, :, KN_ROW])
         kn_ps = psum.tile([P, PACK, P], F32, name="kn_ps", tag="kn_ps")
         for t in range(PACK):
             nc.tensor.transpose(kn_ps[:, t, :], kn_got[:, t : I : PACK], ident[:])
         neg_kn = keep.tile([P, PACK], F32, name="neg_kn")
         nc.scalar.activation(neg_kn[:], kn_ps[:, :, KN_ROW], ACT.Copy, scale=-1.0)
-        a_ps = psum.tile([P, I], F32, name="a_ps")
+        a_ps = psum.tile([P, I], F32, name="a_ps", tag="a_ps")
         nc.tensor.matmul_mx(
             out=a_ps[:], lhsT=q_codes[:].bitcast(FP8X4), lhsT_scale=q_bytes[:],
             rhs=pts_codes[:].bitcast(FP8X4), rhs_scale=pts_plane[:], start=True, stop=True,

@@ -155,7 +155,6 @@ def tile_attend_kernelridge_kernel(tc, query, pts_words, pts_scales, kn, qn, us,
             return o_ps
 
         mid_bf = keep.tile([P, P, PACK], BF16, name="mid_bf", align_bytes=64)
-        last_bf = keep.tile([P, P, PACK], BF16, name="last_bf", align_bytes=64)
 
         got0 = gather(0)
         got1 = gather(1)
@@ -171,12 +170,21 @@ def tile_attend_kernelridge_kernel(tc, query, pts_words, pts_scales, kn, qn, us,
         head = keep.tile([P, 2 * P], F32, name="head")
         nc.scalar.copy(head[:], product(wv_codes[:, Q : Q + 2 * P], wv_plane[:, Q : Q + 2 * P])[:])
         nc.sync.dma_start(out[:, 0 : 2 * P], head[:])
-        values(3, last_bf[:])
+        got3 = gather(3)
+        last_ps = psum_ring.tile([P, 2, P], F32, name="v_ps")
+        for u in range(2):
+            nc.tensor.transpose(last_ps[:, u, :], got3[:].bitcast(F32)[:, u : I // 2 : 2], ident[:])
+        H = P // 2
+        halves = [keep.tile([P, H, PACK], BF16, name="half_bf%d" % h, align_bytes=64) for h in range(2)]
+        for h in range(2):
+            nc.scalar.copy(halves[h][:].bitcast(F32), last_ps[:, :, H * h : H * (h + 1)].rearrange("s u e -> s e u"))
         mid_codes, mid_plane = quantise("mid", mid_bf[:], "coef3", [(0, P)])
         mid = keep.tile([P, P], F32, name="mid")
         nc.scalar.copy(mid[:], product(mid_codes[:], mid_plane[:])[:])
         nc.sync.dma_start(out[:, 2 * P : 3 * P], mid[:])
-        last_codes, last_plane = quantise("last", last_bf[:], "last_codes", [(0, P)])
         last = keep.tile([P, P], F32, name="last")
-        nc.vector.tensor_copy(last[:], product(last_codes[:], last_plane[:])[:])
+        half_q = [quantise("half%d" % h, halves[h][:], "half_codes%d" % h, [(0, H)]) for h in range(2)]
+        half_ps = [product(c[:], s[:]) for c, s in half_q]
+        nc.scalar.copy(last[:, 0:H], half_ps[0][:])
+        nc.vector.tensor_copy(last[:, H:P], half_ps[1][:])
         nc.sync.dma_start(out[:, E - P : E], last[:])

@@ -19,10 +19,13 @@ MULT = mybir.AluOpType.mult
 
 P = 128
 PACK = 4
-KN_ROW = P - 1
-SCALE_ROWS = 16
-SCALE_ROW0 = 48
-E_TILES = E // P
+QUADRANT = 32
+ROWS_PER_QUADRANT = 4
+SCALE_ROWS = D // 32
+SCALE_ROW0 = 2 * QUADRANT - SCALE_ROWS
+LAST_ROW = P - 1
+LINE = 4
+HALF = P // 2
 
 
 def tile_attend_kernelridge_kernel(tc, query, pts_words, pts_scales, kn, qn, us, coef, offs, out):
@@ -51,26 +54,26 @@ def tile_attend_kernelridge_kernel(tc, query, pts_words, pts_scales, kn, qn, us,
         nc.gpsimd.memset(scales[0:SCALE_ROW0, :].bitcast(I32), 0)
         nc.gpsimd.memset(scales[SCALE_ROW0 + SCALE_ROWS : P, :].bitcast(I32), 0)
         nc.gpsimd.memset(pts_plane[:].bitcast(I32), 0)
-        nc.vector.memset(kn_win[0:KN_ROW, :], 0.0)
+        nc.vector.memset(kn_win[0:LAST_ROW, :], 0.0)
         make_identity(nc, ident[:])
-        nc.gpsimd.memset(qn_row[0:KN_ROW, :], 0.0)
-        nc.gpsimd.memset(us_row[0:KN_ROW, :], 0.0)
+        nc.gpsimd.memset(qn_row[0:LAST_ROW, :], 0.0)
+        nc.gpsimd.memset(us_row[0:LAST_ROW, :], 0.0)
 
         nc.sync.dma_start(q_raw[:], query.rearrange("(p t) q -> p t q", t=PACK))
-        nc.scalar.dma_start(kn_win[KN_ROW : KN_ROW + 1, :], kn[0:1, :])
+        nc.scalar.dma_start(kn_win[LAST_ROW:P, :], kn[0:1, :])
         nc.sync.dma_start(offsets[:], offs)
         nc.sync.dma_start(scales[SCALE_ROW0 : SCALE_ROW0 + SCALE_ROWS, :].bitcast(I32), pts_scales[0].bitcast(I32))
-        nc.scalar.dma_start(qn_row[KN_ROW : KN_ROW + 1, :], qn.rearrange("q o -> o q"))
+        nc.scalar.dma_start(qn_row[LAST_ROW:P, :], qn.rearrange("q o -> o q"))
         nc.sync.dma_start(words[:].bitcast(I32), pts_words[0].rearrange("p n t -> p (n t)").bitcast(I32))
-        nc.scalar.dma_start(us_row[KN_ROW : KN_ROW + 1, :], us)
+        nc.scalar.dma_start(us_row[LAST_ROW:P, :], us)
         coef_win = [load_coef(0)]
 
         scale_got = keep.tile([P, I], U8, name="scale_got", align_bytes=64)
         nc.vector.tensor_copy(scale_got[:], scales[:].indirect(offsets[:]))
-        for r in range(4):
+        for r in range(ROWS_PER_QUADRANT):
             nc.sync.dma_start(
-                pts_plane[r:P:32, :].bitcast(I32),
-                scale_got[SCALE_ROW0 + r : SCALE_ROW0 + SCALE_ROWS : 4, :].bitcast(I32),
+                pts_plane[r:P:QUADRANT, :].bitcast(I32),
+                scale_got[SCALE_ROW0 + r : SCALE_ROW0 + SCALE_ROWS : ROWS_PER_QUADRANT, :].bitcast(I32),
             )
         coef_win.append(load_coef(1))
         kn_got = keep.tile([P, I], F32, name="kn_got")
@@ -83,34 +86,34 @@ def tile_attend_kernelridge_kernel(tc, query, pts_words, pts_scales, kn, qn, us,
         coef_win.append(load_coef(2))
         coef_win.append(load_coef(3))
         q_codes = keep.tile([P, Q], U32, name="q_codes", tag="kn_win", align_bytes=64)
-        q_bytes = keep.tile([P, Q], U8, name="q_bytes", align_bytes=64)
-        nc.vector.quantize_mx(out=q_codes[:].bitcast(FP8X4), scales=q_bytes[:], in_=q_bf[:].rearrange("p q t -> p (q t)"))
-
+        q_plane = keep.tile([P, Q], U8, name="q_plane", align_bytes=64)
+        nc.vector.quantize_mx(out=q_codes[:].bitcast(FP8X4), scales=q_plane[:], in_=q_bf[:].rearrange("p q t -> p (q t)"))
 
         qn_ps = psum.tile([P, P], F32, name="qn_ps", tag="a_ps")
         nc.tensor.transpose(qn_ps[:], qn_row[:], ident[:])
         qn_col = keep.tile([P, 1], F32, name="qn_col")
-        nc.scalar.copy(qn_col[:], qn_ps[:, KN_ROW : KN_ROW + 1])
+        nc.scalar.copy(qn_col[:], qn_ps[:, LAST_ROW:P])
         us_ps = psum.tile([P, PACK, P], F32, name="us_ps", tag="gap_ps")
         for t in range(PACK):
-            nc.tensor.transpose(us_ps[:, t, :], us_row[:, t : I : PACK], ident[:])
+            nc.tensor.transpose(us_ps[:, t, :], us_row[:, t:I:PACK], ident[:])
         us_cols = keep.tile([P, PACK], F32, name="us_cols")
-        nc.scalar.copy(us_cols[:], us_ps[:, :, KN_ROW])
+        nc.scalar.copy(us_cols[:], us_ps[:, :, LAST_ROW])
         kn_ps = psum.tile([P, PACK, P], F32, name="kn_ps", tag="kn_ps")
         for t in range(PACK):
-            nc.tensor.transpose(kn_ps[:, t, :], kn_got[:, t : I : PACK], ident[:])
+            nc.tensor.transpose(kn_ps[:, t, :], kn_got[:, t:I:PACK], ident[:])
         neg_kn = keep.tile([P, PACK], F32, name="neg_kn")
-        nc.scalar.activation(neg_kn[:], kn_ps[:, :, KN_ROW], ACT.Copy, scale=-1.0)
+        nc.scalar.activation(neg_kn[:], kn_ps[:, :, LAST_ROW], ACT.Copy, scale=-1.0)
+
         a_ps = psum.tile([P, I], F32, name="a_ps", tag="a_ps")
         nc.tensor.matmul_mx(
-            out=a_ps[:], lhsT=q_codes[:].bitcast(FP8X4), lhsT_scale=q_bytes[:],
+            out=a_ps[:], lhsT=q_codes[:].bitcast(FP8X4), lhsT_scale=q_plane[:],
             rhs=pts_codes[:].bitcast(FP8X4), rhs_scale=pts_plane[:], start=True, stop=True,
         )
-        gap = [keep.tile([P, 2, P], F32, name="gap%d" % h) for h in range(2)]
+        gap = [keep.tile([P, 2, P], F32, name="gap%d" % u) for u in range(2)]
         dealt = a_ps[:].rearrange("q (s t) -> q t s", t=PACK)
-        for h in range(2):
-            nc.scalar.activation(gap[h][:], dealt[:, 2 * h : 2 * h + 2, :], ACT.Identity, bias=qn_col[:], scale=-1.0)
-        gap_ps = [psum.tile([P, 2, Q], F32, name="gap_ps%d" % h, tag=["gap_ps", "kn_ps"][h]) for h in range(2)]
+        for u in range(2):
+            nc.scalar.activation(gap[u][:], dealt[:, 2 * u : 2 * u + 2, :], ACT.Identity, bias=qn_col[:], scale=-1.0)
+        gap_ps = [psum.tile([P, 2, Q], F32, name="gap_ps%d" % u, tag=["gap_ps", "kn_ps"][u]) for u in range(2)]
         for t in range(PACK):
             nc.tensor.transpose(gap_ps[t // 2][:, t % 2, :], gap[t // 2][:, t % 2, :], ident[:])
         gauss = keep.tile([P, PACK, Q], F32, name="gauss")
@@ -122,22 +125,21 @@ def tile_attend_kernelridge_kernel(tc, query, pts_words, pts_scales, kn, qn, us,
             nc.vector.tensor_copy(got[:], coef_win[j][:].indirect(offsets[:]))
             return got
 
-        def values(j, v_bf):
-            turn(j, gather(j), v_bf)
-
-        def turn(j, got, v_bf):
+        def turn(got, v_ps):
             pairs = got[:].bitcast(F32)
-            if j == 0:
-                v_ps = psum.tile([P, 2, P], F32, name="v_ps0", tag="kn_ps")
-            else:
-                v_ps = psum_ring.tile([P, 2, P], F32, name="v_ps")
             for u in range(2):
                 nc.tensor.transpose(v_ps[:, u, :], pairs[:, u : I // 2 : 2], ident[:])
-            nc.scalar.copy(v_bf.bitcast(F32), v_ps[:].rearrange("s u e -> s e u"))
+            return v_ps
 
-        def quantise(name, x_bf, slot, cuts):
+        def weave(v_bf, turned):
+            nc.scalar.copy(v_bf.bitcast(F32), turned.rearrange("s u e -> s e u"))
+
+        def ring_bank():
+            return psum_ring.tile([P, 2, P], F32, name="v_ps")
+
+        def quantise(name, x_bf, tag, cuts):
             width = x_bf.shape[1]
-            codes = keep.tile([P, width], U32, name="codes_" + name, tag=slot, align_bytes=64)
+            codes = keep.tile([P, width], U32, name="codes_" + name, tag=tag, align_bytes=64)
             plane = keep.tile([P, width], U8, name="plane_" + name, align_bytes=64)
             for lo, hi in cuts:
                 nc.vector.quantize_mx(
@@ -160,31 +162,32 @@ def tile_attend_kernelridge_kernel(tc, query, pts_words, pts_scales, kn, qn, us,
         got1 = gather(1)
         wv_bf = keep.tile([P, Q + 2 * P, PACK], BF16, name="wv_bf", tag="coef1", align_bytes=64)
         nc.vector.tensor_tensor(
-            wv_bf[:, 0:Q, :].rearrange("s (c i) t -> s c t i", i=4), gauss[:].rearrange("s t (c i) -> s c t i", i=4),
-            us_cols[:].unsqueeze(1).unsqueeze(3).to_broadcast([P, Q // 4, PACK, 4]), MULT,
+            wv_bf[:, 0:Q, :].rearrange("s (c i) t -> s c t i", i=LINE),
+            gauss[:].rearrange("s t (c i) -> s c t i", i=LINE),
+            us_cols[:].unsqueeze(1).unsqueeze(3).to_broadcast([P, Q // LINE, PACK, LINE]), MULT,
         )
-        turn(0, got0, wv_bf[:, Q : Q + P, :])
-        turn(1, got1, wv_bf[:, Q + P : Q + 2 * P, :])
-        values(2, mid_bf[:])
+        weave(wv_bf[:, Q : Q + P, :], turn(got0, psum.tile([P, 2, P], F32, name="v_ps0", tag="kn_ps"))[:])
+        weave(wv_bf[:, Q + P : Q + 2 * P, :], turn(got1, ring_bank())[:])
+        weave(mid_bf[:], turn(gather(2), ring_bank())[:])
+
         wv_codes, wv_plane = quantise("wv", wv_bf[:], "coef2", [(0, Q + P), (Q + P, Q + 2 * P)])
         head = keep.tile([P, 2 * P], F32, name="head")
         nc.scalar.copy(head[:], product(wv_codes[:, Q : Q + 2 * P], wv_plane[:, Q : Q + 2 * P])[:])
         nc.sync.dma_start(out[:, 0 : 2 * P], head[:])
-        got3 = gather(3)
-        last_ps = psum_ring.tile([P, 2, P], F32, name="v_ps")
-        for u in range(2):
-            nc.tensor.transpose(last_ps[:, u, :], got3[:].bitcast(F32)[:, u : I // 2 : 2], ident[:])
-        H = P // 2
-        halves = [keep.tile([P, H, PACK], BF16, name="half_bf%d" % h, align_bytes=64) for h in range(2)]
+
+        turned = turn(gather(3), ring_bank())
+        half_bf = [keep.tile([P, HALF, PACK], BF16, name="half_bf%d" % h, align_bytes=64) for h in range(2)]
         for h in range(2):
-            nc.scalar.copy(halves[h][:].bitcast(F32), last_ps[:, :, H * h : H * (h + 1)].rearrange("s u e -> s e u"))
+            weave(half_bf[h][:], turned[:, :, HALF * h : HALF * (h + 1)])
+
         mid_codes, mid_plane = quantise("mid", mid_bf[:], "coef3", [(0, P)])
         mid = keep.tile([P, P], F32, name="mid")
         nc.scalar.copy(mid[:], product(mid_codes[:], mid_plane[:])[:])
         nc.sync.dma_start(out[:, 2 * P : 3 * P], mid[:])
+
         last = keep.tile([P, P], F32, name="last")
-        half_q = [quantise("half%d" % h, halves[h][:], "half_codes%d" % h, [(0, H)]) for h in range(2)]
-        half_ps = [product(c[:], s[:]) for c, s in half_q]
-        nc.scalar.copy(last[:, 0:H], half_ps[0][:])
-        nc.vector.tensor_copy(last[:, H:P], half_ps[1][:])
+        half_mx = [quantise("half%d" % h, half_bf[h][:], "half_codes%d" % h, [(0, HALF)]) for h in range(2)]
+        half_ps = [product(codes[:], plane[:]) for codes, plane in half_mx]
+        for h in range(2):
+            nc.vector.tensor_copy(last[:, HALF * h : HALF * (h + 1)], half_ps[h][:])
         nc.sync.dma_start(out[:, E - P : E], last[:])

@@ -25,6 +25,8 @@ SCALE_ROWS = D // 32
 SCALE_ROW0 = 2 * QUADRANT - SCALE_ROWS
 LAST_ROW = P - 1
 LINE = 4
+LIST_ROWS = 16
+SCALAR_COLS = 12
 HALF = P // 2
 
 
@@ -32,12 +34,13 @@ def tile_attend_kernelridge_kernel(tc, query, pts_words, pts_scales, kn, qn, us,
     nc = tc.nc
     with ExitStack() as ctx:
         keep = ctx.enter_context(tc.tile_pool(name="keep", bufs=1))
+        laid = ctx.enter_context(tc.tile_pool(name="laid", bufs=1))
         psum = ctx.enter_context(tc.psum_pool(name="psum", bufs=1))
         psum_out = ctx.enter_context(tc.psum_pool(name="psum_out", bufs=3))
         psum_ring = ctx.enter_context(tc.psum_pool(name="psum_ring", bufs=2))
 
         offsets = keep.tile([P, I // 16], U16, name="offsets")
-        words = keep.tile([P, T], U32, name="words", tag="coef3", align_bytes=64)
+        words = laid.tile([P, T], U32, name="words", offset=0, align_bytes=64)
         scales = keep.tile([P, T], U8, name="scales", tag="coef1", align_bytes=64)
         kn_win = keep.tile([P, T], F32, name="kn_win", tag="kn_win", align_bytes=64)
         pts_plane = keep.tile([P, I], U8, name="pts_plane", align_bytes=64)
@@ -47,7 +50,10 @@ def tile_attend_kernelridge_kernel(tc, query, pts_words, pts_scales, kn, qn, us,
         ident = keep.tile([P, P], F32, name="ident")
 
         def load_coef(j):
-            win = keep.tile([P, T], F32, name="coef_win%d" % j, tag="coef%d" % j, align_bytes=64)
+            if j == 3:
+                win = laid.tile([P, T], F32, name="coef_win3", offset=0, align_bytes=64)
+            else:
+                win = keep.tile([P, T], F32, name="coef_win%d" % j, tag="coef%d" % j, align_bytes=64)
             nc.sync.dma_start(win[:], coef[P * j : P * (j + 1), :])
             return win
 
@@ -121,7 +127,7 @@ def tile_attend_kernelridge_kernel(tc, query, pts_words, pts_scales, kn, qn, us,
             nc.scalar.activation(gauss[:, t, :], gap_ps[t // 2][:, t % 2, :], ACT.Exp, bias=neg_kn[:, t : t + 1], scale=-1.0)
 
         def gather(j):
-            got = keep.tile([P, I], BF16, name="got%d" % j)
+            got = keep.tile([P, I], BF16, name="got%d" % j, tag="got%d" % j)
             nc.vector.tensor_copy(got[:], coef_win[j][:].indirect(offsets[:]))
             return got
 
@@ -156,8 +162,6 @@ def tile_attend_kernelridge_kernel(tc, query, pts_words, pts_scales, kn, qn, us,
             )
             return o_ps
 
-        mid_bf = keep.tile([P, P, PACK], BF16, name="mid_bf", align_bytes=64)
-
         got0 = gather(0)
         got1 = gather(1)
         wv_bf = keep.tile([P, Q + 2 * P, PACK], BF16, name="wv_bf", tag="coef1", align_bytes=64)
@@ -168,19 +172,26 @@ def tile_attend_kernelridge_kernel(tc, query, pts_words, pts_scales, kn, qn, us,
         )
         weave(wv_bf[:, Q : Q + P, :], turn(got0, psum.tile([P, 2, P], F32, name="v_ps0", tag="kn_ps"))[:])
         weave(wv_bf[:, Q + P : Q + 2 * P, :], turn(got1, ring_bank())[:])
-        weave(mid_bf[:], turn(gather(2), ring_bank())[:])
+        turned2 = turn(gather(2), ring_bank())
 
         wv_codes, wv_plane = quantise("wv", wv_bf[:], "coef2", [(0, Q + P), (Q + P, Q + 2 * P)])
-        head = keep.tile([P, 2 * P], F32, name="head")
-        nc.scalar.copy(head[:], product(wv_codes[:, Q : Q + 2 * P], wv_plane[:, Q : Q + 2 * P])[:])
-        nc.sync.dma_start(out[:, 0 : 2 * P], head[:])
+        head_ps = product(wv_codes[:, Q : Q + 2 * P], wv_plane[:, Q : Q + 2 * P])
 
-        turned = turn(gather(3), ring_bank())
+        got3 = keep.tile([P, I], BF16, name="got3", tag="got1")
+        cut = LIST_ROWS * SCALAR_COLS
+        nc.scalar.activation(got3[:, 0:cut], coef_win[3][:].indirect(offsets[:, 0:SCALAR_COLS]), ACT.Copy)
+        nc.vector.tensor_copy(got3[:, cut:I], coef_win[3][:].indirect(offsets[:, SCALAR_COLS : I // LIST_ROWS]))
+        turned = turn(got3, ring_bank())
+        head = laid.tile([P, 2 * P], F32, name="head", offset=0, align_bytes=64)
+        nc.scalar.copy(head[:], head_ps[:])
+        nc.sync.dma_start(out[:, 0 : 2 * P], head[:])
+        mid_bf = laid.tile([P, P, PACK], BF16, name="mid_bf", offset=4 * 2 * P, align_bytes=64)
+        nc.vector.tensor_copy(mid_bf[:].bitcast(F32), turned2[:].rearrange("s u e -> s e u"))
         half_bf = [keep.tile([P, HALF, PACK], BF16, name="half_bf%d" % h, align_bytes=64) for h in range(2)]
         for h in range(2):
             weave(half_bf[h][:], turned[:, :, HALF * h : HALF * (h + 1)])
 
-        mid_codes, mid_plane = quantise("mid", mid_bf[:], "coef3", [(0, P)])
+        mid_codes, mid_plane = quantise("mid", mid_bf[:], "mid_codes", [(0, P)])
         mid = keep.tile([P, P], F32, name="mid")
         nc.scalar.copy(mid[:], product(mid_codes[:], mid_plane[:])[:])
         nc.sync.dma_start(out[:, 2 * P : 3 * P], mid[:])

@@ -26,7 +26,7 @@ SCALE_ROW0 = 2 * QUADRANT - SCALE_ROWS
 LAST_ROW = P - 1
 LINE = 4
 LIST_ROWS = 16
-SCALAR_COLS = 12
+SCALAR_COLS = 16
 HALF = P // 2
 
 

@@ -27,6 +27,7 @@ LAST_ROW = P - 1
 LINE = 4
 LIST_ROWS = 16
 SCALAR_COLS = 16
+WIN_BYTES = 4 * T
 HALF = P // 2
 
 
@@ -44,14 +45,14 @@ def tile_attend_kernelridge_kernel(tc, query, pts_words, pts_scales, kn, qn, us,
         scales = keep.tile([P, T], U8, name="scales", tag="coef1", align_bytes=64)
         kn_win = keep.tile([P, T], F32, name="kn_win", tag="kn_win", align_bytes=64)
         pts_plane = keep.tile([P, I], U8, name="pts_plane", align_bytes=64)
-        q_raw = keep.tile([P, PACK, Q], F32, name="q_raw", tag="coef2", align_bytes=64)
+        q_raw = laid.tile([P, PACK, Q], F32, name="q_raw", offset=WIN_BYTES, align_bytes=64)
         us_row = keep.tile([P, I], F32, name="us_row")
         qn_row = keep.tile([P, Q], F32, name="qn_row")
         ident = keep.tile([P, P], F32, name="ident")
 
         def load_coef(j):
-            if j == 3:
-                win = laid.tile([P, T], F32, name="coef_win3", offset=0, align_bytes=64)
+            if j >= 2:
+                win = laid.tile([P, T], F32, name="coef_win%d" % j, offset=WIN_BYTES * (3 - j), align_bytes=64)
             else:
                 win = keep.tile([P, T], F32, name="coef_win%d" % j, tag="coef%d" % j, align_bytes=64)
             nc.sync.dma_start(win[:], coef[P * j : P * (j + 1), :])
@@ -131,6 +132,13 @@ def tile_attend_kernelridge_kernel(tc, query, pts_words, pts_scales, kn, qn, us,
             nc.vector.tensor_copy(got[:], coef_win[j][:].indirect(offsets[:]))
             return got
 
+        def shared_gather(j, tag):
+            got = keep.tile([P, I], BF16, name="got%d" % j, tag=tag)
+            cut = LIST_ROWS * SCALAR_COLS
+            nc.scalar.activation(got[:, 0:cut], coef_win[j][:].indirect(offsets[:, 0:SCALAR_COLS]), ACT.Copy)
+            nc.vector.tensor_copy(got[:, cut:I], coef_win[j][:].indirect(offsets[:, SCALAR_COLS : I // LIST_ROWS]))
+            return got
+
         def turn(got, v_ps):
             pairs = got[:].bitcast(F32)
             for u in range(2):
@@ -164,37 +172,42 @@ def tile_attend_kernelridge_kernel(tc, query, pts_words, pts_scales, kn, qn, us,
 
         got0 = gather(0)
         got1 = gather(1)
-        wv_bf = keep.tile([P, Q + 2 * P, PACK], BF16, name="wv_bf", tag="coef1", align_bytes=64)
+        wv_bf = keep.tile([P, Q + P, PACK], BF16, name="wv_bf", tag="coef1", align_bytes=64)
         nc.vector.tensor_tensor(
             wv_bf[:, 0:Q, :].rearrange("s (c i) t -> s c t i", i=LINE),
             gauss[:].rearrange("s t (c i) -> s c t i", i=LINE),
             us_cols[:].unsqueeze(1).unsqueeze(3).to_broadcast([P, Q // LINE, PACK, LINE]), MULT,
         )
         weave(wv_bf[:, Q : Q + P, :], turn(got0, psum.tile([P, 2, P], F32, name="v_ps0", tag="kn_ps"))[:])
-        weave(wv_bf[:, Q + P : Q + 2 * P, :], turn(got1, ring_bank())[:])
-        turned2 = turn(gather(2), ring_bank())
+        turned1 = turn(got1, ring_bank())
+        turned2 = turn(shared_gather(2, "got2"), ring_bank())
+        v1_bf = laid.tile([P, P, PACK], BF16, name="v1_bf", offset=WIN_BYTES, align_bytes=64)
+        weave(v1_bf[:], turned1[:])
 
-        wv_codes, wv_plane = quantise("wv", wv_bf[:], "coef2", [(0, Q + P), (Q + P, Q + 2 * P)])
+        wv_codes = laid.tile([P, Q + 2 * P], U32, name="wv_codes", offset=WIN_BYTES + 2 * PACK * P, align_bytes=64)
+        wv_plane = keep.tile([P, Q + 2 * P], U8, name="wv_plane", align_bytes=64)
+        for lo, x_bf in ((0, wv_bf), (Q + P, v1_bf)):
+            hi = lo + x_bf.shape[1]
+            nc.vector.quantize_mx(
+                out=wv_codes[:, lo:hi].bitcast(FP8X4), scales=wv_plane[:, lo:hi], in_=x_bf[:].rearrange("s c t -> s (c t)"),
+            )
         head_ps = product(wv_codes[:, Q : Q + 2 * P], wv_plane[:, Q : Q + 2 * P])
+        mid_bf = keep.tile([P, P, PACK], BF16, name="mid_bf", align_bytes=64)
+        weave(mid_bf[:], turned2[:])
 
-        got3 = keep.tile([P, I], BF16, name="got3", tag="got1")
-        cut = LIST_ROWS * SCALAR_COLS
-        nc.scalar.activation(got3[:, 0:cut], coef_win[3][:].indirect(offsets[:, 0:SCALAR_COLS]), ACT.Copy)
-        nc.vector.tensor_copy(got3[:, cut:I], coef_win[3][:].indirect(offsets[:, SCALAR_COLS : I // LIST_ROWS]))
-        turned = turn(got3, ring_bank())
-        head = laid.tile([P, 2 * P], F32, name="head", offset=0, align_bytes=64)
-        nc.scalar.copy(head[:], head_ps[:])
-        nc.sync.dma_start(out[:, 0 : 2 * P], head[:])
-        mid_bf = laid.tile([P, P, PACK], BF16, name="mid_bf", offset=4 * 2 * P, align_bytes=64)
-        nc.vector.tensor_copy(mid_bf[:].bitcast(F32), turned2[:].rearrange("s u e -> s e u"))
+        turned = turn(shared_gather(3, "got1"), ring_bank())
+        head = laid.tile([P, 3 * P], F32, name="head", offset=0, align_bytes=64)
+        mid_codes = laid.tile([P, P], U32, name="mid_codes", offset=4 * 3 * P, align_bytes=64)
+        mid_plane = keep.tile([P, P], U8, name="mid_plane", align_bytes=64)
+        nc.vector.quantize_mx(out=mid_codes[:].bitcast(FP8X4), scales=mid_plane[:], in_=mid_bf[:].rearrange("s c t -> s (c t)"))
+        mid_ps = product(mid_codes[:], mid_plane[:])
+        nc.vector.tensor_copy(head[:, 0 : 2 * P], head_ps[:])
         half_bf = [keep.tile([P, HALF, PACK], BF16, name="half_bf%d" % h, align_bytes=64) for h in range(2)]
         for h in range(2):
             weave(half_bf[h][:], turned[:, :, HALF * h : HALF * (h + 1)])
 
-        mid_codes, mid_plane = quantise("mid", mid_bf[:], "mid_codes", [(0, P)])
-        mid = keep.tile([P, P], F32, name="mid")
-        nc.scalar.copy(mid[:], product(mid_codes[:], mid_plane[:])[:])
-        nc.sync.dma_start(out[:, 2 * P : 3 * P], mid[:])
+        nc.scalar.copy(head[:, 2 * P : 3 * P], mid_ps[:])
+        nc.sync.dma_start(out[:, 0 : 3 * P], head[:])
 
         last = keep.tile([P, P], F32, name="last")
         half_mx = [quantise("half%d" % h, half_bf[h][:], "half_codes%d" % h, [(0, HALF)]) for h in range(2)]

@@ -202,12 +202,13 @@ def tile_attend_kernelridge_kernel(tc, query, pts_words, pts_scales, kn, qn, us,
         nc.vector.quantize_mx(out=mid_codes[:].bitcast(FP8X4), scales=mid_plane[:], in_=mid_bf[:].rearrange("s c t -> s (c t)"))
         mid_ps = product(mid_codes[:], mid_plane[:])
         nc.vector.tensor_copy(head[:, 0 : 2 * P], head_ps[:])
+        nc.sync.dma_start(out[:, 0 : 2 * P], head[:, 0 : 2 * P])
         half_bf = [keep.tile([P, HALF, PACK], BF16, name="half_bf%d" % h, align_bytes=64) for h in range(2)]
         for h in range(2):
             weave(half_bf[h][:], turned[:, :, HALF * h : HALF * (h + 1)])
 
         nc.scalar.copy(head[:, 2 * P : 3 * P], mid_ps[:])
-        nc.sync.dma_start(out[:, 0 : 3 * P], head[:])
+        nc.sync.dma_start(out[:, 2 * P : 3 * P], head[:, 2 * P : 3 * P])
 
         last = keep.tile([P, P], F32, name="last")
         half_mx = [quantise("half%d" % h, half_bf[h][:], "half_codes%d" % h, [(0, HALF)]) for h in range(2)]

@@ -28,6 +28,8 @@ LINE = 4
 LIST_ROWS = 16
 SCALAR_COLS = 16
 WIN_BYTES = 4 * T
+WIN3_AT = I
+WIN2_AT = WIN_BYTES + I
 HALF = P // 2
 
 
@@ -45,14 +47,14 @@ def tile_attend_kernelridge_kernel(tc, query, pts_words, pts_scales, kn, qn, us,
         scales = keep.tile([P, T], U8, name="scales", tag="coef1", align_bytes=64)
         kn_win = keep.tile([P, T], F32, name="kn_win", tag="kn_win", align_bytes=64)
         pts_plane = keep.tile([P, I], U8, name="pts_plane", align_bytes=64)
-        q_raw = laid.tile([P, PACK, Q], F32, name="q_raw", offset=WIN_BYTES, align_bytes=64)
+        q_raw = laid.tile([P, PACK, Q], F32, name="q_raw", offset=WIN2_AT, align_bytes=64)
         us_row = keep.tile([P, I], F32, name="us_row")
         qn_row = keep.tile([P, Q], F32, name="qn_row")
         ident = keep.tile([P, P], F32, name="ident")
 
         def load_coef(j):
             if j >= 2:
-                win = laid.tile([P, T], F32, name="coef_win%d" % j, offset=WIN_BYTES * (3 - j), align_bytes=64)
+                win = laid.tile([P, T], F32, name="coef_win%d" % j, offset=[WIN2_AT, WIN3_AT][j - 2], align_bytes=64)
             else:
                 win = keep.tile([P, T], F32, name="coef_win%d" % j, tag="coef%d" % j, align_bytes=64)
             nc.sync.dma_start(win[:], coef[P * j : P * (j + 1), :])
@@ -75,7 +77,7 @@ def tile_attend_kernelridge_kernel(tc, query, pts_words, pts_scales, kn, qn, us,
         nc.scalar.dma_start(us_row[LAST_ROW:P, :], us)
         coef_win = [load_coef(0)]
 
-        scale_got = keep.tile([P, I], U8, name="scale_got", align_bytes=64)
+        scale_got = laid.tile([P, I], U8, name="scale_got", offset=WIN_BYTES, align_bytes=64)
         nc.vector.tensor_copy(scale_got[:], scales[:].indirect(offsets[:]))
         for r in range(ROWS_PER_QUADRANT):
             nc.sync.dma_start(
@@ -181,10 +183,10 @@ def tile_attend_kernelridge_kernel(tc, query, pts_words, pts_scales, kn, qn, us,
         weave(wv_bf[:, Q : Q + P, :], turn(got0, psum.tile([P, 2, P], F32, name="v_ps0", tag="kn_ps"))[:])
         turned1 = turn(got1, ring_bank())
         turned2 = turn(shared_gather(2, "got2"), ring_bank())
-        v1_bf = laid.tile([P, P, PACK], BF16, name="v1_bf", offset=WIN_BYTES, align_bytes=64)
+        v1_bf = laid.tile([P, P, PACK], BF16, name="v1_bf", offset=WIN2_AT, align_bytes=64)
         weave(v1_bf[:], turned1[:])
 
-        wv_codes = laid.tile([P, Q + 2 * P], U32, name="wv_codes", offset=WIN_BYTES + 2 * PACK * P, align_bytes=64)
+        wv_codes = laid.tile([P, Q + 2 * P], U32, name="wv_codes", offset=WIN2_AT + 2 * PACK * P, align_bytes=64)
         wv_plane = keep.tile([P, Q + 2 * P], U8, name="wv_plane", align_bytes=64)
         for lo, x_bf in ((0, wv_bf), (Q + P, v1_bf)):
             hi = lo + x_bf.shape[1]
@@ -196,8 +198,8 @@ def tile_attend_kernelridge_kernel(tc, query, pts_words, pts_scales, kn, qn, us,
         weave(mid_bf[:], turned2[:])
 
         turned = turn(shared_gather(3, "got1"), ring_bank())
-        head = laid.tile([P, 3 * P], F32, name="head", offset=0, align_bytes=64)
-        mid_codes = laid.tile([P, P], U32, name="mid_codes", offset=4 * 3 * P, align_bytes=64)
+        head = laid.tile([P, 3 * P], F32, name="head", offset=WIN3_AT, align_bytes=64)
+        mid_codes = laid.tile([P, P], U32, name="mid_codes", offset=WIN3_AT + 4 * 3 * P, align_bytes=64)
         mid_plane = keep.tile([P, P], U8, name="mid_plane", align_bytes=64)
         nc.vector.quantize_mx(out=mid_codes[:].bitcast(FP8X4), scales=mid_plane[:], in_=mid_bf[:].rearrange("s c t -> s (c t)"))
         mid_ps = product(mid_codes[:], mid_plane[:])

@@ -62,19 +62,19 @@ def tile_attend_kernelridge_kernel(tc, query, pts_words, pts_scales, kn, qn, us,
 
         nc.gpsimd.memset(scales[0:SCALE_ROW0, :].bitcast(I32), 0)
         nc.gpsimd.memset(scales[SCALE_ROW0 + SCALE_ROWS : P, :].bitcast(I32), 0)
-        nc.gpsimd.memset(pts_plane[:].bitcast(I32), 0)
+        nc.gpsimd.dma_start(qn_row[LAST_ROW:P, :], qn.rearrange("q o -> o q"))
+        nc.gpsimd.dma_start(us_row[LAST_ROW:P, :], us)
         nc.vector.memset(kn_win[0:LAST_ROW, :], 0.0)
+        nc.vector.memset(pts_plane[:].bitcast(I32), 0)
+        nc.vector.memset(qn_row[0:LAST_ROW, :], 0.0)
+        nc.vector.memset(us_row[0:LAST_ROW, :], 0.0)
         make_identity(nc, ident[:])
-        nc.gpsimd.memset(qn_row[0:LAST_ROW, :], 0.0)
-        nc.gpsimd.memset(us_row[0:LAST_ROW, :], 0.0)
 
         nc.sync.dma_start(q_raw[:], query.rearrange("(p t) q -> p t q", t=PACK))
         nc.scalar.dma_start(kn_win[LAST_ROW:P, :], kn[0:1, :])
         nc.sync.dma_start(offsets[:], offs)
         nc.sync.dma_start(scales[SCALE_ROW0 : SCALE_ROW0 + SCALE_ROWS, :].bitcast(I32), pts_scales[0].bitcast(I32))
-        nc.scalar.dma_start(qn_row[LAST_ROW:P, :], qn.rearrange("q o -> o q"))
         nc.sync.dma_start(words[:].bitcast(I32), pts_words[0].rearrange("p n t -> p (n t)").bitcast(I32))
-        nc.scalar.dma_start(us_row[LAST_ROW:P, :], us)
         coef_win = [load_coef(0)]
 
         scale_got = laid.tile([P, I], U8, name="scale_got", offset=WIN_BYTES, align_bytes=64)

@@ -60,14 +60,6 @@ def tile_attend_kernelridge_kernel(tc, query, pts_words, pts_scales, kn, qn, us,
             nc.sync.dma_start(win[:], coef[P * j : P * (j + 1), :])
             return win
 
-        nc.gpsimd.memset(scales[0:SCALE_ROW0, :].bitcast(I32), 0)
-        nc.gpsimd.memset(scales[SCALE_ROW0 + SCALE_ROWS : P, :].bitcast(I32), 0)
-        nc.gpsimd.dma_start(qn_row[LAST_ROW:P, :], qn.rearrange("q o -> o q"))
-        nc.gpsimd.dma_start(us_row[LAST_ROW:P, :], us)
-        nc.vector.memset(kn_win[0:LAST_ROW, :], 0.0)
-        nc.vector.memset(pts_plane[:].bitcast(I32), 0)
-        nc.vector.memset(qn_row[0:LAST_ROW, :], 0.0)
-        nc.vector.memset(us_row[0:LAST_ROW, :], 0.0)
         make_identity(nc, ident[:])
 
         nc.sync.dma_start(q_raw[:], query.rearrange("(p t) q -> p t q", t=PACK))
@@ -75,6 +67,15 @@ def tile_attend_kernelridge_kernel(tc, query, pts_words, pts_scales, kn, qn, us,
         nc.sync.dma_start(offsets[:], offs)
         nc.sync.dma_start(scales[SCALE_ROW0 : SCALE_ROW0 + SCALE_ROWS, :].bitcast(I32), pts_scales[0].bitcast(I32))
         nc.sync.dma_start(words[:].bitcast(I32), pts_words[0].rearrange("p n t -> p (n t)").bitcast(I32))
+        nc.gpsimd.dma_start(qn_row[LAST_ROW:P, :], qn.rearrange("q o -> o q"))
+        nc.gpsimd.dma_start(us_row[LAST_ROW:P, :], us)
+
+        nc.vector.memset(scales[0:SCALE_ROW0, :].bitcast(I32), 0)
+        nc.vector.memset(scales[SCALE_ROW0 + SCALE_ROWS : P, :].bitcast(I32), 0)
+        nc.vector.memset(pts_plane[:].bitcast(I32), 0)
+        nc.vector.memset(kn_win[0:LAST_ROW, :], 0.0)
+        nc.gpsimd.memset(qn_row[0:LAST_ROW, :], 0.0)
+        nc.gpsimd.memset(us_row[0:LAST_ROW, :], 0.0)
         coef_win = [load_coef(0)]
 
         scale_got = laid.tile([P, I], U8, name="scale_got", offset=WIN_BYTES, align_bytes=64)
@@ -98,20 +99,20 @@ def tile_attend_kernelridge_kernel(tc, query, pts_words, pts_scales, kn, qn, us,
         q_plane = keep.tile([P, Q], U8, name="q_plane", align_bytes=64)
         nc.vector.quantize_mx(out=q_codes[:].bitcast(FP8X4), scales=q_plane[:], in_=q_bf[:].rearrange("p q t -> p (q t)"))
 
-        qn_ps = psum.tile([P, P], F32, name="qn_ps", tag="a_ps")
-        nc.tensor.transpose(qn_ps[:], qn_row[:], ident[:])
-        qn_col = keep.tile([P, 1], F32, name="qn_col")
-        nc.scalar.copy(qn_col[:], qn_ps[:, LAST_ROW:P])
-        us_ps = psum.tile([P, PACK, P], F32, name="us_ps", tag="gap_ps")
-        for t in range(PACK):
-            nc.tensor.transpose(us_ps[:, t, :], us_row[:, t:I:PACK], ident[:])
-        us_cols = keep.tile([P, PACK], F32, name="us_cols")
-        nc.scalar.copy(us_cols[:], us_ps[:, :, LAST_ROW])
         kn_ps = psum.tile([P, PACK, P], F32, name="kn_ps", tag="kn_ps")
         for t in range(PACK):
             nc.tensor.transpose(kn_ps[:, t, :], kn_got[:, t:I:PACK], ident[:])
         neg_kn = keep.tile([P, PACK], F32, name="neg_kn")
         nc.scalar.activation(neg_kn[:], kn_ps[:, :, LAST_ROW], ACT.Copy, scale=-1.0)
+        qn_ps = psum.tile([P, P], F32, name="qn_ps", tag="a_ps")
+        nc.tensor.transpose(qn_ps[:], qn_row[:], ident[:])
+        qn_col = keep.tile([P, 1], F32, name="qn_col")
+        nc.scalar.copy(qn_col[:], qn_ps[:, LAST_ROW:P])
+        us_ps = psum_ring.tile([P, PACK, P], F32, name="us_ps", tag="v_ps")
+        for t in range(PACK):
+            nc.tensor.transpose(us_ps[:, t, :], us_row[:, t:I:PACK], ident[:])
+        us_cols = keep.tile([P, PACK], F32, name="us_cols")
+        nc.scalar.copy(us_cols[:], us_ps[:, :, LAST_ROW])
 
         a_ps = psum.tile([P, I], F32, name="a_ps", tag="a_ps")
         nc.tensor.matmul_mx(
@@ -151,7 +152,7 @@ def tile_attend_kernelridge_kernel(tc, query, pts_words, pts_scales, kn, qn, us,
             nc.scalar.copy(v_bf.bitcast(F32), turned.rearrange("s u e -> s e u"))
 
         def ring_bank():
-            return psum_ring.tile([P, 2, P], F32, name="v_ps")
+            return psum_ring.tile([P, 2, P], F32, name="v_ps", tag="v_ps")
 
         def quantise(name, x_bf, tag, cuts):
             width = x_bf.shape[1]

@@ -30,6 +30,7 @@ SCALAR_COLS = 16
 WIN_BYTES = 4 * T
 WIN3_AT = I
 WIN2_AT = WIN_BYTES + I
+WIN1_AT = WIN2_AT + WIN_BYTES
 HALF = P // 2
 
 
@@ -44,7 +45,7 @@ def tile_attend_kernelridge_kernel(tc, query, pts_words, pts_scales, kn, qn, us,
 
         offsets = keep.tile([P, I // 16], U16, name="offsets")
         words = laid.tile([P, T], U32, name="words", offset=0, align_bytes=64)
-        scales = keep.tile([P, T], U8, name="scales", tag="coef1", align_bytes=64)
+        scales = laid.tile([P, T], U8, name="scales", offset=WIN1_AT, align_bytes=64)
         kn_win = keep.tile([P, T], F32, name="kn_win", tag="kn_win", align_bytes=64)
         pts_plane = keep.tile([P, I], U8, name="pts_plane", align_bytes=64)
         q_raw = laid.tile([P, PACK, Q], F32, name="q_raw", offset=WIN2_AT, align_bytes=64)
@@ -53,8 +54,8 @@ def tile_attend_kernelridge_kernel(tc, query, pts_words, pts_scales, kn, qn, us,
         ident = keep.tile([P, P], F32, name="ident")
 
         def load_coef(j):
-            if j >= 2:
-                win = laid.tile([P, T], F32, name="coef_win%d" % j, offset=[WIN2_AT, WIN3_AT][j - 2], align_bytes=64)
+            if j >= 1:
+                win = laid.tile([P, T], F32, name="coef_win%d" % j, offset=[WIN1_AT, WIN2_AT, WIN3_AT][j - 1], align_bytes=64)
             else:
                 win = keep.tile([P, T], F32, name="coef_win%d" % j, tag="coef%d" % j, align_bytes=64)
             nc.sync.dma_start(win[:], coef[P * j : P * (j + 1), :])
@@ -87,7 +88,7 @@ def tile_attend_kernelridge_kernel(tc, query, pts_words, pts_scales, kn, qn, us,
             )
         coef_win.append(load_coef(1))
         kn_got = keep.tile([P, I], F32, name="kn_got")
-        nc.vector.tensor_copy(kn_got[:], kn_win[:].indirect(offsets[:]))
+        nc.scalar.activation(kn_got[:], kn_win[:].indirect(offsets[:]), ACT.Copy)
         pts_codes = keep.tile([P, I], U32, name="pts_codes", align_bytes=64)
         nc.vector.tensor_copy(pts_codes[:], words[:].indirect(offsets[:]))
 
@@ -104,21 +105,16 @@ def tile_attend_kernelridge_kernel(tc, query, pts_words, pts_scales, kn, qn, us,
             nc.tensor.transpose(kn_ps[:, t, :], kn_got[:, t:I:PACK], ident[:])
         neg_kn = keep.tile([P, PACK], F32, name="neg_kn")
         nc.scalar.activation(neg_kn[:], kn_ps[:, :, LAST_ROW], ACT.Copy, scale=-1.0)
-        qn_ps = psum.tile([P, P], F32, name="qn_ps", tag="a_ps")
-        nc.tensor.transpose(qn_ps[:], qn_row[:], ident[:])
-        qn_col = keep.tile([P, 1], F32, name="qn_col")
-        nc.scalar.copy(qn_col[:], qn_ps[:, LAST_ROW:P])
-        us_ps = psum_ring.tile([P, PACK, P], F32, name="us_ps", tag="v_ps")
-        for t in range(PACK):
-            nc.tensor.transpose(us_ps[:, t, :], us_row[:, t:I:PACK], ident[:])
-        us_cols = keep.tile([P, PACK], F32, name="us_cols")
-        nc.scalar.copy(us_cols[:], us_ps[:, :, LAST_ROW])
 
         a_ps = psum.tile([P, I], F32, name="a_ps", tag="a_ps")
         nc.tensor.matmul_mx(
             out=a_ps[:], lhsT=q_codes[:].bitcast(FP8X4), lhsT_scale=q_plane[:],
             rhs=pts_codes[:].bitcast(FP8X4), rhs_scale=pts_plane[:], start=True, stop=True,
         )
+        qn_ps = psum.tile([P, P], F32, name="qn_ps", tag="gap_ps")
+        nc.tensor.transpose(qn_ps[:], qn_row[:], ident[:])
+        qn_col = keep.tile([P, 1], F32, name="qn_col")
+        nc.scalar.copy(qn_col[:], qn_ps[:, LAST_ROW:P])
         gap = [keep.tile([P, 2, P], F32, name="gap%d" % u) for u in range(2)]
         dealt = a_ps[:].rearrange("q (s t) -> q t s", t=PACK)
         for u in range(2):
@@ -126,6 +122,9 @@ def tile_attend_kernelridge_kernel(tc, query, pts_words, pts_scales, kn, qn, us,
         gap_ps = [psum.tile([P, 2, Q], F32, name="gap_ps%d" % u, tag=["gap_ps", "kn_ps"][u]) for u in range(2)]
         for t in range(PACK):
             nc.tensor.transpose(gap_ps[t // 2][:, t % 2, :], gap[t // 2][:, t % 2, :], ident[:])
+        us_ps = psum.tile([P, PACK, P], F32, name="us_ps", tag="a_ps")
+        for t in range(PACK):
+            nc.tensor.transpose(us_ps[:, t, :], us_row[:, t:I:PACK], ident[:])
         gauss = keep.tile([P, PACK, Q], F32, name="gauss")
         for t in range(PACK):
             nc.scalar.activation(gauss[:, t, :], gap_ps[t // 2][:, t % 2, :], ACT.Exp, bias=neg_kn[:, t : t + 1], scale=-1.0)
@@ -175,14 +174,16 @@ def tile_attend_kernelridge_kernel(tc, query, pts_words, pts_scales, kn, qn, us,
 
         got0 = gather(0)
         got1 = gather(1)
-        wv_bf = keep.tile([P, Q + P, PACK], BF16, name="wv_bf", tag="coef1", align_bytes=64)
+        us_cols = laid.tile([P, PACK], F32, name="us_cols", offset=WIN1_AT + 2 * PACK * (Q + P), align_bytes=64)
+        nc.vector.tensor_copy(us_cols[:], us_ps[:, :, LAST_ROW])
+        wv_bf = laid.tile([P, Q + P, PACK], BF16, name="wv_bf", offset=WIN1_AT, align_bytes=64)
         nc.vector.tensor_tensor(
             wv_bf[:, 0:Q, :].rearrange("s (c i) t -> s c t i", i=LINE),
             gauss[:].rearrange("s t (c i) -> s c t i", i=LINE),
             us_cols[:].unsqueeze(1).unsqueeze(3).to_broadcast([P, Q // LINE, PACK, LINE]), MULT,
         )
         weave(wv_bf[:, Q : Q + P, :], turn(got0, psum.tile([P, 2, P], F32, name="v_ps0", tag="kn_ps"))[:])
-        turned1 = turn(got1, ring_bank())
+        turned1 = turn(got1, psum.tile([P, 2, P], F32, name="v_ps1", tag="gap_ps"))
         turned2 = turn(shared_gather(2, "got2"), ring_bank())
         v1_bf = laid.tile([P, P, PACK], BF16, name="v1_bf", offset=WIN2_AT, align_bytes=64)
         weave(v1_bf[:], turned1[:])

@@ -64,9 +64,9 @@ def tile_attend_kernelridge_kernel(tc, query, pts_words, pts_scales, kn, qn, us,
         make_identity(nc, ident[:])
 
         nc.sync.dma_start(q_raw[:], query.rearrange("(p t) q -> p t q", t=PACK))
-        nc.scalar.dma_start(kn_win[LAST_ROW:P, :], kn[0:1, :])
         nc.sync.dma_start(offsets[:], offs)
         nc.sync.dma_start(scales[SCALE_ROW0 : SCALE_ROW0 + SCALE_ROWS, :].bitcast(I32), pts_scales[0].bitcast(I32))
+        nc.sync.dma_start(kn_win[LAST_ROW:P, :], kn[0:1, :])
         nc.sync.dma_start(words[:].bitcast(I32), pts_words[0].rearrange("p n t -> p (n t)").bitcast(I32))
         nc.gpsimd.dma_start(qn_row[LAST_ROW:P, :], qn.rearrange("q o -> o q"))
         nc.gpsimd.dma_start(us_row[LAST_ROW:P, :], us)

@@ -123,8 +123,10 @@ def tile_attend_kernelridge_kernel(tc, query, pts_words, pts_scales, kn, qn, us,
         for t in range(PACK):
             nc.tensor.transpose(gap_ps[t // 2][:, t % 2, :], gap[t // 2][:, t % 2, :], ident[:])
         us_ps = psum.tile([P, PACK, P], F32, name="us_ps", tag="a_ps")
+        us_dealt = keep.tile([P, PACK, P], F32, name="us_dealt")
+        nc.gpsimd.tensor_copy(us_dealt[:], us_row[:].rearrange("p (s t) -> p t s", t=PACK))
         for t in range(PACK):
-            nc.tensor.transpose(us_ps[:, t, :], us_row[:, t:I:PACK], ident[:])
+            nc.tensor.transpose(us_ps[:, t, :], us_dealt[:, t, :], ident[:])
         gauss = keep.tile([P, PACK, Q], F32, name="gauss")
         for t in range(PACK):
             nc.scalar.activation(gauss[:, t, :], gap_ps[t // 2][:, t % 2, :], ACT.Exp, bias=neg_kn[:, t : t + 1], scale=-1.0)
@@ -174,13 +176,11 @@ def tile_attend_kernelridge_kernel(tc, query, pts_words, pts_scales, kn, qn, us,
 
         got0 = gather(0)
         got1 = gather(1)
-        us_cols = laid.tile([P, PACK], F32, name="us_cols", offset=WIN1_AT + 2 * PACK * (Q + P), align_bytes=64)
-        nc.vector.tensor_copy(us_cols[:], us_ps[:, :, LAST_ROW])
         wv_bf = laid.tile([P, Q + P, PACK], BF16, name="wv_bf", offset=WIN1_AT, align_bytes=64)
         nc.vector.tensor_tensor(
             wv_bf[:, 0:Q, :].rearrange("s (c i) t -> s c t i", i=LINE),
             gauss[:].rearrange("s t (c i) -> s c t i", i=LINE),
-            us_cols[:].unsqueeze(1).unsqueeze(3).to_broadcast([P, Q // LINE, PACK, LINE]), MULT,
+            us_ps[:, :, LAST_ROW:P].unsqueeze(1).to_broadcast([P, Q // LINE, PACK, LINE]), MULT,
         )
         weave(wv_bf[:, Q : Q + P, :], turn(got0, psum.tile([P, 2, P], F32, name="v_ps0", tag="kn_ps"))[:])
         turned1 = turn(got1, psum.tile([P, 2, P], F32, name="v_ps1", tag="gap_ps"))

from contextlib import ExitStack

import concourse.mybir as mybir
from concourse.masks import make_identity

D, T, I, Q, E = 512, 2048, 512, 128, 512
FLOPS = 2 * Q * I * D + 2 * Q * I * E
BYTES = 4 * D * Q + D * T + 16 * T + 4 * T + 4 * Q + 4 * I + 4 * E * T + 2 * 128 * 32 + 4 * Q * E

F32 = mybir.dt.float32
BF16 = mybir.dt.bfloat16
I32 = mybir.dt.int32
U32 = mybir.dt.uint32
U16 = mybir.dt.uint16
U8 = mybir.dt.uint8
FP8X4 = mybir.dt.float8_e4m3fn_x4
ACT = mybir.ActivationFunctionType
MULT = mybir.AluOpType.mult

P = 128
PACK = 4
QUADRANT = 32
ROWS_PER_QUADRANT = 4
SCALE_ROWS = D // 32
SCALE_ROW0 = 2 * QUADRANT - SCALE_ROWS
LAST_ROW = P - 1
LINE = 4
LIST_ROWS = 16
SCALAR_COLS = 16
WIN_BYTES = 4 * T
WIN3_AT = I
WIN2_AT = WIN_BYTES + I
WIN1_AT = WIN2_AT + WIN_BYTES
HALF = P // 2


def tile_attend_kernelridge_kernel(tc, query, pts_words, pts_scales, kn, qn, us, coef, offs, out):
    nc = tc.nc
    with ExitStack() as ctx:
        keep = ctx.enter_context(tc.tile_pool(name="keep", bufs=1))
        laid = ctx.enter_context(tc.tile_pool(name="laid", bufs=1))
        psum = ctx.enter_context(tc.psum_pool(name="psum", bufs=1))
        psum_out = ctx.enter_context(tc.psum_pool(name="psum_out", bufs=3))
        psum_ring = ctx.enter_context(tc.psum_pool(name="psum_ring", bufs=2))

        offsets = keep.tile([P, I // 16], U16, name="offsets")
        words = laid.tile([P, T], U32, name="words", offset=0, align_bytes=64)
        scales = laid.tile([P, T], U8, name="scales", offset=WIN1_AT, align_bytes=64)
        kn_win = keep.tile([P, T], F32, name="kn_win", tag="kn_win", align_bytes=64)
        pts_plane = keep.tile([P, I], U8, name="pts_plane", align_bytes=64)
        q_raw = laid.tile([P, PACK, Q], F32, name="q_raw", offset=WIN2_AT, align_bytes=64)
        us_row = keep.tile([P, I], F32, name="us_row")
        qn_row = keep.tile([P, Q], F32, name="qn_row")
        ident = keep.tile([P, P], F32, name="ident")

        def load_coef(j):
            if j >= 1:
                win = laid.tile([P, T], F32, name="coef_win%d" % j, offset=[WIN1_AT, WIN2_AT, WIN3_AT][j - 1], align_bytes=64)
            else:
                win = keep.tile([P, T], F32, name="coef_win%d" % j, tag="coef%d" % j, align_bytes=64)
            nc.sync.dma_start(win[:], coef[P * j : P * (j + 1), :])
            return win

        make_identity(nc, ident[:])

        nc.sync.dma_start(q_raw[:], query.rearrange("(p t) q -> p t q", t=PACK))
        nc.sync.dma_start(offsets[:], offs)
        nc.sync.dma_start(scales[SCALE_ROW0 : SCALE_ROW0 + SCALE_ROWS, :].bitcast(I32), pts_scales[0].bitcast(I32))
        nc.sync.dma_start(kn_win[LAST_ROW:P, :], kn[0:1, :])
        nc.sync.dma_start(words[:].bitcast(I32), pts_words[0].rearrange("p n t -> p (n t)").bitcast(I32))
        nc.gpsimd.dma_start(qn_row[LAST_ROW:P, :], qn.rearrange("q o -> o q"))
        nc.gpsimd.dma_start(us_row[LAST_ROW:P, :], us)

        nc.vector.memset(scales[0:SCALE_ROW0, :].bitcast(I32), 0)
        nc.vector.memset(scales[SCALE_ROW0 + SCALE_ROWS : P, :].bitcast(I32), 0)
        nc.vector.memset(pts_plane[:].bitcast(I32), 0)
        nc.vector.memset(kn_win[0:LAST_ROW, :], 0.0)
        nc.gpsimd.memset(qn_row[0:LAST_ROW, :], 0.0)
        nc.gpsimd.memset(us_row[0:LAST_ROW, :], 0.0)
        coef_win = [load_coef(0)]

        scale_got = laid.tile([P, I], U8, name="scale_got", offset=WIN_BYTES, align_bytes=64)
        nc.vector.tensor_copy(scale_got[:], scales[:].indirect(offsets[:]))
        for r in range(ROWS_PER_QUADRANT):
            nc.sync.dma_start(
                pts_plane[r:P:QUADRANT, :].bitcast(I32),
                scale_got[SCALE_ROW0 + r : SCALE_ROW0 + SCALE_ROWS : ROWS_PER_QUADRANT, :].bitcast(I32),
            )
        coef_win.append(load_coef(1))
        kn_got = keep.tile([P, I], F32, name="kn_got")
        nc.scalar.activation(kn_got[:], kn_win[:].indirect(offsets[:]), ACT.Copy)
        pts_codes = keep.tile([P, I], U32, name="pts_codes", align_bytes=64)
        nc.vector.tensor_copy(pts_codes[:], words[:].indirect(offsets[:]))

        q_bf = keep.tile([P, Q, PACK], BF16, name="q_bf", align_bytes=64)
        nc.scalar.activation(q_bf[:], q_raw[:].rearrange("p t q -> p q t"), ACT.Copy)
        coef_win.append(load_coef(2))
        coef_win.append(load_coef(3))
        q_codes = keep.tile([P, Q], U32, name="q_codes", tag="kn_win", align_bytes=64)
        q_plane = keep.tile([P, Q], U8, name="q_plane", align_bytes=64)
        nc.vector.quantize_mx(out=q_codes[:].bitcast(FP8X4), scales=q_plane[:], in_=q_bf[:].rearrange("p q t -> p (q t)"))

        kn_ps = psum.tile([P, PACK, P], F32, name="kn_ps", tag="kn_ps")
        for t in range(PACK):
            nc.tensor.transpose(kn_ps[:, t, :], kn_got[:, t:I:PACK], ident[:])
        neg_kn = keep.tile([P, PACK], F32, name="neg_kn")
        nc.scalar.activation(neg_kn[:], kn_ps[:, :, LAST_ROW], ACT.Copy, scale=-1.0)

        a_ps = psum.tile([P, I], F32, name="a_ps", tag="a_ps")
        nc.tensor.matmul_mx(
            out=a_ps[:], lhsT=q_codes[:].bitcast(FP8X4), lhsT_scale=q_plane[:],
            rhs=pts_codes[:].bitcast(FP8X4), rhs_scale=pts_plane[:], start=True, stop=True,
        )
        qn_ps = psum.tile([P, P], F32, name="qn_ps", tag="gap_ps")
        nc.tensor.transpose(qn_ps[:], qn_row[:], ident[:])
        qn_col = keep.tile([P, 1], F32, name="qn_col")
        nc.scalar.copy(qn_col[:], qn_ps[:, LAST_ROW:P])
        gap = [keep.tile([P, 2, P], F32, name="gap%d" % u) for u in range(2)]
        dealt = a_ps[:].rearrange("q (s t) -> q t s", t=PACK)
        for u in range(2):
            nc.scalar.activation(gap[u][:], dealt[:, 2 * u : 2 * u + 2, :], ACT.Identity, bias=qn_col[:], scale=-1.0)
        gap_ps = [psum.tile([P, 2, Q], F32, name="gap_ps%d" % u, tag=["gap_ps", "kn_ps"][u]) for u in range(2)]
        for t in range(PACK):
            nc.tensor.transpose(gap_ps[t // 2][:, t % 2, :], gap[t // 2][:, t % 2, :], ident[:])
        us_ps = psum.tile([P, PACK, P], F32, name="us_ps", tag="a_ps")
        us_dealt = keep.tile([P, PACK, P], F32, name="us_dealt")
        nc.gpsimd.tensor_copy(us_dealt[:], us_row[:].rearrange("p (s t) -> p t s", t=PACK))
        for t in range(PACK):
            nc.tensor.transpose(us_ps[:, t, :], us_dealt[:, t, :], ident[:])
        gauss = keep.tile([P, PACK, Q], F32, name="gauss")
        for t in range(PACK):
            nc.scalar.activation(gauss[:, t, :], gap_ps[t // 2][:, t % 2, :], ACT.Exp, bias=neg_kn[:, t : t + 1], scale=-1.0)

        def gather(j):
            got = keep.tile([P, I], BF16, name="got%d" % j, tag="got%d" % j)
            nc.vector.tensor_copy(got[:], coef_win[j][:].indirect(offsets[:]))
            return got

        def shared_gather(j, tag):
            got = keep.tile([P, I], BF16, name="got%d" % j, tag=tag)
            cut = LIST_ROWS * SCALAR_COLS
            nc.scalar.activation(got[:, 0:cut], coef_win[j][:].indirect(offsets[:, 0:SCALAR_COLS]), ACT.Copy)
            nc.vector.tensor_copy(got[:, cut:I], coef_win[j][:].indirect(offsets[:, SCALAR_COLS : I // LIST_ROWS]))
            return got

        def turn(got, v_ps):
            pairs = got[:].bitcast(F32)
            for u in range(2):
                nc.tensor.transpose(v_ps[:, u, :], pairs[:, u : I // 2 : 2], ident[:])
            return v_ps

        def weave(v_bf, turned):
            nc.scalar.copy(v_bf.bitcast(F32), turned.rearrange("s u e -> s e u"))

        def ring_bank():
            return psum_ring.tile([P, 2, P], F32, name="v_ps", tag="v_ps")

        def quantise(name, x_bf, tag, cuts):
            width = x_bf.shape[1]
            codes = keep.tile([P, width], U32, name="codes_" + name, tag=tag, align_bytes=64)
            plane = keep.tile([P, width], U8, name="plane_" + name, align_bytes=64)
            for lo, hi in cuts:
                nc.vector.quantize_mx(
                    out=codes[:, lo:hi].bitcast(FP8X4), scales=plane[:, lo:hi],
                    in_=x_bf[:, lo:hi, :].rearrange("s c t -> s (c t)"),
                )
            return codes, plane

        def product(v_codes, v_plane):
            o_ps = psum_out.tile([P, v_codes.shape[1]], F32, name="o_ps")
            nc.tensor.matmul_mx(
                out=o_ps[:], lhsT=wv_codes[:, 0:Q].bitcast(FP8X4), lhsT_scale=wv_plane[:, 0:Q],
                rhs=v_codes.bitcast(FP8X4), rhs_scale=v_plane, start=True, stop=True,
            )
            return o_ps

        got0 = gather(0)
        got1 = gather(1)
        wv_bf = laid.tile([P, Q + P, PACK], BF16, name="wv_bf", offset=WIN1_AT, align_bytes=64)
        nc.vector.tensor_tensor(
            wv_bf[:, 0:Q, :].rearrange("s (c i) t -> s c t i", i=LINE),
            gauss[:].rearrange("s t (c i) -> s c t i", i=LINE),
            us_ps[:, :, LAST_ROW:P].unsqueeze(1).to_broadcast([P, Q // LINE, PACK, LINE]), MULT,
        )
        weave(wv_bf[:, Q : Q + P, :], turn(got0, psum.tile([P, 2, P], F32, name="v_ps0", tag="kn_ps"))[:])
        turned1 = turn(got1, psum.tile([P, 2, P], F32, name="v_ps1", tag="gap_ps"))
        turned2 = turn(shared_gather(2, "got2"), ring_bank())
        v1_bf = laid.tile([P, P, PACK], BF16, name="v1_bf", offset=WIN2_AT, align_bytes=64)
        weave(v1_bf[:], turned1[:])

        wv_codes = laid.tile([P, Q + 2 * P], U32, name="wv_codes", offset=WIN2_AT + 2 * PACK * P, align_bytes=64)
        wv_plane = keep.tile([P, Q + 2 * P], U8, name="wv_plane", align_bytes=64)
        for lo, x_bf in ((0, wv_bf), (Q + P, v1_bf)):
            hi = lo + x_bf.shape[1]
            nc.vector.quantize_mx(
                out=wv_codes[:, lo:hi].bitcast(FP8X4), scales=wv_plane[:, lo:hi], in_=x_bf[:].rearrange("s c t -> s (c t)"),
            )
        head_ps = product(wv_codes[:, Q : Q + 2 * P], wv_plane[:, Q : Q + 2 * P])
        mid_bf = keep.tile([P, P, PACK], BF16, name="mid_bf", align_bytes=64)
        weave(mid_bf[:], turned2[:])

        turned = turn(shared_gather(3, "got1"), ring_bank())
        head = laid.tile([P, 3 * P], F32, name="head", offset=WIN3_AT, align_bytes=64)
        mid_codes = laid.tile([P, P], U32, name="mid_codes", offset=WIN3_AT + 4 * 3 * P, align_bytes=64)
        mid_plane = keep.tile([P, P], U8, name="mid_plane", align_bytes=64)
        nc.vector.quantize_mx(out=mid_codes[:].bitcast(FP8X4), scales=mid_plane[:], in_=mid_bf[:].rearrange("s c t -> s (c t)"))
        mid_ps = product(mid_codes[:], mid_plane[:])
        nc.vector.tensor_copy(head[:, 0 : 2 * P], head_ps[:])
        nc.sync.dma_start(out[:, 0 : 2 * P], head[:, 0 : 2 * P])
        half_bf = [keep.tile([P, HALF, PACK], BF16, name="half_bf%d" % h, align_bytes=64) for h in range(2)]
        for h in range(2):
            weave(half_bf[h][:], turned[:, :, HALF * h : HALF * (h + 1)])

        nc.scalar.copy(head[:, 2 * P : 3 * P], mid_ps[:])
        nc.sync.dma_start(out[:, 2 * P : 3 * P], head[:, 2 * P : 3 * P])

        last = keep.tile([P, P], F32, name="last")
        half_mx = [quantise("half%d" % h, half_bf[h][:], "half_codes%d" % h, [(0, HALF)]) for h in range(2)]
        half_ps = [product(codes[:], plane[:]) for codes, plane in half_mx]
        for h in range(2):
            nc.vector.tensor_copy(last[:, HALF * h : HALF * (h + 1)], half_ps[h][:])
        nc.sync.dma_start(out[:, E - P : E], last[:])
